import numpy as np
import ml_dtypes


def mxq(x, axis, fmt="e4m3"):
    dtype, down = {"e4m3": (ml_dtypes.float8_e4m3fn, 7), "e5m2": (ml_dtypes.float8_e5m2, 14)}[fmt]
    v = np.moveaxis(np.asarray(x, np.float32).astype(ml_dtypes.bfloat16).astype(np.float64), axis, -1)
    blocks = v.reshape(v.shape[:-1] + (-1, 32))
    amax = np.abs(blocks).max(-1, keepdims=True)
    byte = np.maximum(np.where(amax > 0, np.frexp(amax)[1] - 1 + 127, 0) - down, 1)
    scale = np.exp2(byte - 127.0)
    codes = (blocks / scale).astype(np.float32).astype(dtype).astype(np.float64)
    return np.moveaxis((codes * scale).reshape(v.shape), -1, axis)


WIDE = False


def mx_kscale(k):
    if not WIDE:
        return np.ones(k)
    levels = np.array([10, -10, 5, -5, 0])
    if k % 512:
        return np.exp2(np.random.permutation(np.resize(levels, k // 32))).repeat(32)
    a = np.empty((k // 512, 16))
    for p in range(k // 512):
        a[p, :8] = np.random.permutation(np.resize(levels, 8))
        for g in range(8):
            far = levels[np.abs(levels - a[p, g]) >= 10]
            a[p, g + 8] = far[np.random.randint(len(far))]
    return np.exp2(a.ravel()).repeat(32)


BF16 = ml_dtypes.bfloat16


def bf(x):
    return np.asarray(x, np.float32).astype(BF16)


def f64(x):
    return np.asarray(x).astype(np.float64)


E2M1 = np.array([0.0, 0.5, 1.0, 1.5, 2.0, 3.0, 4.0, 6.0, -0.0, -0.5, -1.0, -1.5, -2.0, -3.0, -4.0, -6.0])


def pack_weight(w, fmt):
    k, n = w.shape
    w = f64(bf(w)).reshape(k // 32, 32, n)
    amax = np.abs(w).max(1)
    if fmt == "e4m3":
        byte = np.frexp(amax)[1] - 1 + 127 - 7
    else:
        mant, ex = np.frexp(amax / 6.0)
        byte = np.where(mant > 0.5, ex, ex - 1) + 127
    byte = np.clip(np.where(amax > 0, byte, 1), 1, 254)
    scaled = (w * np.exp2(127.0 - byte)[:, None, :]).reshape(k, n).astype(np.float32)
    by_word = np.ascontiguousarray(scaled.reshape(k // 512, 128, 4, n).transpose(0, 1, 3, 2))
    if fmt == "e4m3":
        words = by_word.astype(ml_dtypes.float8_e4m3fn).view(np.uint8)
    else:
        c = by_word.astype(ml_dtypes.float4_e2m1fn).view(np.uint8) & 0xF
        words = c[..., 0::2] | (c[..., 1::2] << 4)
    return np.ascontiguousarray(words), np.ascontiguousarray(byte.astype(np.uint8).reshape(k // 512, 16, n))


def unpack_weight(words, scales, fmt):
    g, p, n, _ = words.shape
    if fmt == "e4m3":
        vals = np.ascontiguousarray(words).view(ml_dtypes.float8_e4m3fn).astype(np.float64)
    else:
        nib = np.empty((g, p, n, 4), np.uint8)
        nib[..., 0::2] = words & 0xF
        nib[..., 1::2] = words >> 4
        vals = E2M1[nib]
    vals = vals * np.repeat(np.exp2(scales.astype(np.float64) - 127.0), 8, axis=1)[..., None]
    return vals.transpose(0, 1, 3, 2).reshape(g * 512, n)
def pack4(w):
    words, scales = pack_weight(w, "e2m1")
    return words.reshape(words.shape[0], 128, -1), scales


def unpack4(words, scales):
    return unpack_weight(words.reshape(words.shape[0], 128, -1, 2), scales, "e2m1")


def planes(Y):
    n, m = Y.shape
    b = f64(bf(Y)).reshape(n // 32, 32, m)
    amax = np.abs(b).max(1)
    byte = np.clip(np.where(amax > 0, np.frexp(amax)[1] - 1 + 127 - 7, 1), 1, 254)
    codes = (b * np.exp2(127.0 - byte)[:, None, :]).reshape(n, m).astype(np.float32).astype(ml_dtypes.float8_e4m3fn).view(np.uint8)
    words = codes.reshape(n // 512, 128, 4, m).transpose(0, 1, 3, 2)
    return np.ascontiguousarray(words), np.ascontiguousarray(byte.astype(np.uint8).reshape(n // 512, 16, m))


MA, R, N, J = 4096, 1024, 2048, 512


def setup_inputs():
    s = mx_kscale(MA)
    t = mx_kscale(R)
    F = np.random.randn(MA, R) * s[:, None] * t[None, :]
    U = np.random.randn(MA, J) / np.sqrt(MA) / s[:, None]
    f_words, f_scales = pack4(F)
    u_words, u_scales = pack4(U)
    spread = np.exp(0.7 * np.random.randn(N, 1))
    e = bf(spread * np.random.randn(N, R) / np.sqrt(R) / t[None, :])
    d = bf(np.exp(0.3 * np.random.randn(R)))
    v = bf(spread * np.random.randn(N, J + 1))
    alpha = bf(np.exp(0.3 * np.random.randn(J)))
    beta = bf(0.6 * np.exp(0.3 * np.random.randn(J)))
    return {"f_words": f_words, "f_scales": f_scales, "u_words": u_words, "u_scales": u_scales,
            "d": d, "e": e, "v": v, "alpha": alpha, "beta": beta}

def reference(f_words, f_scales, u_words, u_scales, d, e, v, alpha, beta):
    F = unpack4(f_words, f_scales)
    U = unpack4(u_words, u_scales)
    h = (F.T @ U) * f64(d)[:, None]
    atu = mxq(f64(e), 1, "e4m3") @ mxq(h, 0, "e4m3")
    V = f64(v)
    y = atu - V[:, :J] * f64(alpha)[None, :] - V[:, 1:] * f64(beta)[None, :]
    Y = y.reshape(N, J)
    words, scales = planes(Y)
    return y, words, scales

@@ -1,0 +1,507 @@
+from contextlib import ExitStack
+
+import concourse.mybir as mybir
+from concourse.masks import make_identity
+
+MA, R, N, J = 4096, 1024, 2048, 512
+FLOPS = 2 * MA * R * J + 2 * N * R * J
+
+F32 = mybir.dt.float32
+BF16 = mybir.dt.bfloat16
+I32 = mybir.dt.int32
+U32 = mybir.dt.uint32
+U8 = mybir.dt.uint8
+FP8X4 = mybir.dt.float8_e4m3fn_x4
+FP4X4 = mybir.dt.float4_e2m1fn_x4
+MULT = mybir.AluOpType.mult
+ADD = mybir.AluOpType.add
+SUB = mybir.AluOpType.subtract
+
+P = 128
+KG = MA // 512
+RH = R // 512
+NG = N // 512
+JT = J // P
+VW = J + 1
+SECOND_BUFS = 8
+SORTED = (0, 1,)
+H_BANKS = ((2, 3, 4, 5), (6, 0, 1, 2))
+
+
+def tile_golub_kahan_defect_k5_kernel(
+    tc, f_words, f_scales, u_words, u_scales, d, e, v, alpha, beta, out_0, out_1, out_2
+):
+    nc = tc.nc
+    with ExitStack() as ctx:
+        keep = ctx.enter_context(tc.tile_pool(name="keep", bufs=1))
+        psum = ctx.enter_context(tc.psum_pool(name="psum", bufs=1))
+        ctx.enter_context(tc.manual_schedule())
+
+        def sb(name, shape, dtype):
+            return keep.tile(shape, dtype, name=name, align_bytes=256 if dtype in (U8, U32) else 64)
+
+        banks = [psum.tile([P, 512], F32, name="bank%d" % b) for b in range(8)]
+
+        vec_rows = sb("vec_rows", [P, P], BF16)
+        vec_cols = sb("vec_cols", [P, 16], BF16)
+        ident_b = sb("ident_b", [P, P], BF16)
+        ident_f = sb("ident_f", [P, P], F32)
+        d_wide = sb("d_wide", [P, R], BF16)
+        ab_sb = sb("ab_sb", [P, 2 * J], BF16)
+        u_w = sb("u_w", [P, KG, 2 * J], U8)
+        u_s = sb("u_s", [P, KG, J], U8)
+        f_w = [sb("f_w%d" % h, [P, KG, 1024], U8) for h in range(RH)]
+        f_s = [sb("f_s%d" % h, [P, KG, 512], U8) for h in range(RH)]
+        v_sb = [sb("v_sb%d" % g, [P, 4 * VW], BF16) for g in range(NG)]
+        e_sb = [sb("e_sb%d" % g, [P, 4, R], BF16) for g in range(NG)]
+        e_codes = [sb("e_codes%d" % g, [P, RH, 512], U32) for g in range(NG)]
+        e_scale = [sb("e_scale%d" % g, [P, RH, 512], U8) for g in range(NG)]
+        hd_t = [sb("hd_t%d" % jt, [P, R], BF16) for jt in range(JT)]
+        hd_in = [sb("hd_in%d" % h, [P, 4 * J], BF16) for h in range(RH)]
+        hd_codes = [sb("hd_codes%d" % h, [P, J], U32) for h in range(RH)]
+        hd_scale = [sb("hd_scale%d" % h, [P, J], U8) for h in range(RH)]
+        y = [sb("y%d" % g, [P, 4, J], F32) for g in range(NG)]
+        second = [sb("second%d" % i, [P, J], F32) for i in range(SECOND_BUFS)]
+        e_in = [sb("e_in%d" % i, [P, 2048], BF16) for i in range(4)]
+        e_sorted = [sb("e_sorted%d" % g, [P, 4, RH, 256], F32) for g in range(2)]
+        y_in = [sb("y_in%d" % i, [P, 256, 4], BF16) for i in range(4)]
+        y_codes = sb("y_codes", [P, NG, J], U32)
+        y_scale = sb("y_scale", [P, NG, J], U8)
+
+        def load_vector(which):
+            vec, r0, r1 = ((alpha, 0, 4), (beta, 4, 8), (d, 8, 16))[which]
+            nc.sync.dma_start(out=vec_rows[r0:r1, :], in_=vec.rearrange("(c p) -> c p", p=P))
+
+        def load_v(g):
+            rows = v[512 * g : 512 * (g + 1), :].rearrange("(p t) j -> p (t j)", t=4)
+            nc.sync.dma_start(out=v_sb[g][:], in_=rows)
+
+        def load_e(g):
+            rows = e[512 * g : 512 * (g + 1), :].rearrange("(p t) r -> p t r", t=4)
+            nc.sync.dma_start(out=e_sb[g][:], in_=rows)
+
+        def load_u_words(g0, g1):
+            src = u_words.bitcast(I32)[g0:g1].rearrange("g p c -> p g c")
+            nc.sync.dma_start(out=u_w[:, g0:g1, :].bitcast(I32), in_=src)
+
+        def load_f_words(h, g0, g1):
+            src = f_words.bitcast(I32)[g0:g1, :, 256 * h : 256 * (h + 1)].rearrange("g p c -> p g c")
+            nc.sync.dma_start(out=f_w[h][:, g0:g1, :].bitcast(I32), in_=src)
+
+        planes = [(u_s, u_scales, 0), (f_s[0], f_scales, 0), (f_s[1], f_scales, 128)]
+
+        def clear_plane(which, g0, g1):
+            nc.vector.memset(planes[which][0][:, g0:g1, :].bitcast(I32), 0)
+
+        def load_scales(which, g0, g1):
+            plane, scales, c0 = planes[which]
+            src = scales.bitcast(I32).rearrange("g (q r) c -> r q g c", r=4)
+            for r in range(4):
+                nc.sync.dma_start(out=plane[r:P:32, g0:g1, :].bitcast(I32), in_=src[r][:, g0:g1, c0 : c0 + 128])
+
+        def clear_vectors():
+            nc.vector.memset(vec_rows[:], 0.0)
+
+        def identity(which):
+            make_identity(nc, (ident_b, ident_f)[which][:])
+
+        turned = banks[0][:].bitcast(BF16)
+        ab = banks[7][:].bitcast(BF16)
+        d_ps = banks[1][:].bitcast(BF16)
+
+        def turn_vectors():
+            nc.tensor.transpose(turned[:, 0:P], vec_rows[:], ident_b[:])
+
+        def copy_vectors():
+            nc.scalar.copy(out=vec_cols[:], in_=turned[:, 0:16])
+
+        def spread(which):
+            dst = ab if which == 0 else d_ps
+            for c in range(8):
+                col = vec_cols[:, 8 * which + c : 8 * which + c + 1]
+                nc.tensor.transpose(dst[:, P * c : P * (c + 1)], col.to_broadcast([P, P]), ident_b[:])
+
+        def copy_ab():
+            nc.scalar.copy(out=ab_sb[:], in_=ab)
+
+        def copy_d():
+            for h in range(RH):
+                nc.scalar.copy(
+                    out=d_wide[:, 512 * h : 512 * (h + 1)].rearrange("q (u p e) -> q u p e", u=2, e=2),
+                    in_=d_ps[:, 512 * h : 512 * (h + 1)].rearrange("q (p u e) -> q u p e", u=2, e=2),
+                )
+
+        def vb_products(engine, g, t):
+            v0 = v_sb[g][:, VW * t : VW * t + J]
+            v1 = v_sb[g][:, VW * t + 1 : VW * t + 1 + J]
+            eng, wide = (nc.gpsimd, ab_sb[:]) if engine == "gpsimd" else (nc.vector, ab)
+            eng.tensor_tensor(out=y[g][:, t, :], in0=v0, in1=wide[:, 0:J], op=MULT)
+            eng.tensor_tensor(out=second[(4 * g + t) % SECOND_BUFS][:], in0=v1, in1=wide[:, J : 2 * J], op=MULT)
+
+        def vb_add(g, t):
+            nc.gpsimd.tensor_tensor(
+                out=y[g][:, t, :], in0=y[g][:, t, :], in1=second[(4 * g + t) % SECOND_BUFS][:], op=ADD
+            )
+
+        def first(h, jts, gs):
+            for g in gs:
+                for jt in jts:
+                    nc.tensor.matmul_mx(
+                        out=banks[H_BANKS[h][jt]][:],
+                        lhsT=u_w[:, g, 256 * jt : 256 * (jt + 1)].bitcast(FP4X4),
+                        lhsT_scale=u_s[:, g, P * jt : P * (jt + 1)],
+                        rhs=f_w[h][:, g, :].bitcast(FP4X4),
+                        rhs_scale=f_s[h][:, g, :],
+                        start=(g == 0),
+                        stop=(g == KG - 1),
+                    )
+
+        def scale_by_d(h, jt):
+            cols = slice(512 * h, 512 * (h + 1))
+            nc.vector.tensor_tensor(
+                out=hd_t[jt][:, cols].rearrange("q (u p e) -> q u p e", u=2, e=2),
+                in0=banks[H_BANKS[h][jt]][:].rearrange("q (p u e) -> q u p e", u=2, e=2),
+                in1=d_wide[:, cols].rearrange("q (u p e) -> q u p e", u=2, e=2),
+                op=MULT,
+            )
+
+        def turn_hd(b, h, jt0, jt1):
+            for jt in range(jt0, jt1):
+                words = hd_t[jt][:, 512 * h : 512 * (h + 1)].bitcast(F32)
+                for u in range(2):
+                    slot = 2 * (jt - jt0) + u
+                    nc.tensor.transpose(
+                        banks[b][:, P * slot : P * (slot + 1)], words[:, P * u : P * (u + 1)], ident_f[:]
+                    )
+
+        def copy_hd(b, h, jt0, jt1):
+            n = jt1 - jt0
+            dst = hd_in[h][:].bitcast(F32)[:, 256 * jt0 : 256 * jt1]
+            nc.scalar.copy(
+                out=dst.rearrange("p (i j u) -> p i j u", i=n, u=2),
+                in_=banks[b][:, 0 : 256 * n].rearrange("p (i u j) -> p i j u", i=n, u=2),
+            )
+
+        def quantize_hd(h, jt0, jt1):
+            nc.vector.quantize_mx(
+                out=hd_codes[h][:, P * jt0 : P * jt1].bitcast(FP8X4),
+                scales=hd_scale[h][:, P * jt0 : P * jt1],
+                in_=hd_in[h][:, 512 * jt0 : 512 * jt1],
+            )
+
+        def sort_e(g, h):
+            words = e_sb[g][:].bitcast(F32)[:, :, 256 * h : 256 * (h + 1)]
+            nc.scalar.copy(
+                out=e_sorted[g][:, :, h, :].rearrange("n t (u p) -> n t u p", u=2),
+                in_=words.rearrange("n t (p u) -> n t u p", u=2),
+            )
+
+        def turn_e(b, g, h, pair):
+            for i in range(2):
+                t = 2 * pair + i
+                for u in range(2):
+                    if g in SORTED:
+                        src = e_sorted[g][:, t, h, P * u : P * (u + 1)]
+                    else:
+                        src = e_sb[g][:, t, :].bitcast(F32)[:, 256 * h + u : 256 * (h + 1) : 2]
+                    slot = 2 * i + u
+                    nc.tensor.transpose(banks[b][:, P * slot : P * (slot + 1)], src, ident_f[:])
+
+        def copy_e(b, g, h, pair):
+            dst = e_in[(2 * g + h) % 4][:].bitcast(F32)[:, 512 * pair : 512 * (pair + 1)]
+            nc.scalar.copy(
+                out=dst.rearrange("p (i n u) -> p i n u", i=2, u=2),
+                in_=banks[b][:].rearrange("p (i u n) -> p i n u", i=2, u=2),
+            )
+
+        def quantize_e(g, h):
+            nc.vector.quantize_mx(
+                out=e_codes[g][:, h, :].bitcast(FP8X4), scales=e_scale[g][:, h, :], in_=e_in[(2 * g + h) % 4][:]
+            )
+
+        def second_product(b, g, t0, t1, j0, j1):
+            width = j1 - j0
+            for t in range(t0, t1):
+                for h in range(RH):
+                    nc.tensor.matmul_mx(
+                        out=banks[b][:, width * (t - t0) : width * (t - t0 + 1)],
+                        lhsT=e_codes[g][:, h, P * t : P * (t + 1)].bitcast(FP8X4),
+                        lhsT_scale=e_scale[g][:, h, P * t : P * (t + 1)],
+                        rhs=hd_codes[h][:, j0:j1].bitcast(FP8X4),
+                        rhs_scale=hd_scale[h][:, j0:j1],
+                        start=(h == 0),
+                        stop=(h == RH - 1),
+                    )
+
+        def subtract(b, g, t0, t1, j0, j1):
+            dst = y[g][:, t0:t1, j0:j1]
+            nc.vector.tensor_tensor(out=dst, in0=banks[b][:].rearrange("p (t j) -> p t j", t=t1 - t0), in1=dst, op=SUB)
+
+        def round_y(engine, g, j0, j1):
+            dst = y_in[(2 * g + j0 // 256) % 4][:, j0 % 256 : j0 % 256 + j1 - j0, :]
+            src = y[g][:, :, j0:j1].rearrange("p t j -> p j t")
+            if engine == "scalar":
+                nc.scalar.copy(out=dst, in_=src)
+            elif engine == "vector":
+                nc.vector.tensor_copy(out=dst, in_=src)
+            else:
+                nc.gpsimd.tensor_scalar(out=dst, in0=src, scalar1=1.0, scalar2=0.0, op0=MULT, op1=ADD)
+
+        def quantize_y(g, j0, j1):
+            src = y_in[(2 * g + j0 // 256) % 4][:, j0 % 256 : j0 % 256 + j1 - j0, :]
+            nc.vector.quantize_mx(
+                out=y_codes[:, g, j0:j1].bitcast(FP8X4),
+                scales=y_scale[:, g, j0:j1],
+                in_=src.rearrange("p j t -> p (j t)"),
+            )
+
+        def store_y(g, t0, t1, j0, j1):
+            rows = out_0[512 * g : 512 * (g + 1), :].rearrange("(p t) j -> p t j", t=4)
+            nc.sync.dma_start(out=rows[:, t0:t1, j0:j1], in_=y[g][:, t0:t1, j0:j1])
+
+        def store_words(g, j0, j1):
+            dst = out_1[g].rearrange("p m t -> p (m t)").bitcast(I32)
+            nc.sync.dma_start(out=dst[:, j0:j1], in_=y_codes[:, g, j0:j1].bitcast(I32))
+
+        def store_scales(queue, r, g0, g1):
+            dst = out_2.bitcast(I32).rearrange("g (q r) c -> r q g c", r=4)
+            eng = nc.scalar if queue == "scalar" else nc.sync
+            eng.dma_start(out=dst[r][:, g0:g1, :], in_=y_scale[r:P:32, g0:g1, :].bitcast(I32))
+
+        clear_vectors()
+        clear_plane(0, 0, 3)
+        load_vector(0)
+        clear_plane(0, 3, 8)
+        load_vector(1)
+        load_vector(2)
+        load_u_words(0, 2)
+        clear_plane(1, 3, 8)
+        load_scales(0, 0, 3)
+        clear_plane(1, 0, 3)
+        clear_plane(2, 0, 8)
+        identity(0)
+        load_scales(1, 0, 3)
+        identity(1)
+        turn_vectors()
+        copy_vectors()
+        load_f_words(0, 0, 2)
+        spread(0)
+        load_v(0)
+        load_u_words(2, 4)
+        load_f_words(0, 2, 4)
+        spread(1)
+        copy_ab()
+        load_scales(0, 3, 8)
+        copy_d()
+        load_scales(1, 3, 8)
+        first(0, (0, 1, 2, 3), (0,))
+        vb_products("vector", 0, 1)
+        vb_products("vector", 0, 3)
+        vb_add(0, 1)
+        first(0, (0, 1, 2, 3), (1,))
+        load_u_words(4, 6)
+        load_f_words(0, 4, 6)
+        load_v(1)
+        vb_products("vector", 0, 0)
+        load_u_words(6, 8)
+        vb_add(0, 3)
+        first(0, (0, 1, 2, 3), (2,))
+        load_f_words(0, 6, 8)
+        load_scales(2, 0, 8)
+        vb_products("vector", 0, 2)
+        first(0, (0, 1, 2, 3), (3,))
+        load_f_words(1, 0, 4)
+        vb_add(0, 2)
+        first(0, (0, 1, 2, 3), (4,))
+        load_v(2)
+        vb_products("vector", 1, 2)
+        vb_add(0, 0)
+        first(0, (0, 1, 2, 3), (5,))
+        load_f_words(1, 4, 8)
+        vb_products("vector", 1, 1)
+        load_e(0)
+        first(0, (3,), (6, 7))
+        vb_add(1, 2)
+        load_v(3)
+        first(0, (1,), (6, 7))
+        load_e(1)
+        scale_by_d(0, 3)
+        load_e(2)
+        first(0, (2,), (6, 7))
+        vb_add(1, 1)
+        load_e(3)
+        scale_by_d(0, 1)
+        first(0, (0,), (6, 7))
+        scale_by_d(0, 2)
+        vb_products("gpsimd", 1, 3)
+        scale_by_d(0, 0)
+        first(1, (0, 1, 2, 3), (0,))
+        vb_products("vector", 1, 0)
+        turn_hd(4, 0, 2, 4)
+        turn_hd(3, 0, 0, 2)
+        vb_products("vector", 2, 2)
+        copy_hd(4, 0, 2, 4)
+        first(1, (0, 1, 2, 3), (1,))
+        vb_products("gpsimd", 2, 3)
+        copy_hd(3, 0, 0, 2)
+        vb_products("vector", 2, 1)
+        first(1, (0, 1, 2, 3), (2,))
+        vb_products("vector", 2, 0)
+        first(1, (0, 1, 2, 3), (3,))
+        sort_e(0, 1)
+        vb_add(1, 3)
+        first(1, (3,), (4, 5, 6, 7))
+        vb_products("vector", 3, 3)
+        sort_e(0, 0)
+        vb_add(2, 2)
+        first(1, (1,), (4, 5, 6, 7))
+        vb_products("vector", 3, 1)
+        vb_add(1, 0)
+        first(1, (0,), (4, 5, 6, 7))
+        sort_e(1, 1)
+        scale_by_d(1, 3)
+        vb_add(2, 3)
+        scale_by_d(1, 1)
+        first(1, (2,), (4, 5, 6, 7))
+        sort_e(1, 0)
+        quantize_hd(0, 0, 4)
+        turn_e(5, 0, 0, 0)
+        scale_by_d(1, 0)
+        vb_add(3, 1)
+        turn_e(3, 0, 0, 1)
+        copy_e(5, 0, 0, 0)
+        scale_by_d(1, 2)
+        turn_e(4, 0, 1, 0)
+        turn_hd(6, 1, 0, 2)
+        copy_e(3, 0, 0, 1)
+        vb_products("vector", 3, 0)
+        vb_add(2, 0)
+        turn_e(5, 0, 1, 1)
+        turn_hd(1, 1, 3, 4)
+        copy_e(4, 0, 1, 0)
+        turn_hd(0, 1, 2, 3)
+        turn_e(3, 1, 0, 0)
+        copy_e(5, 0, 1, 1)
+        turn_e(4, 1, 1, 1)
+        quantize_e(0, 0)
+        copy_hd(6, 1, 0, 2)
+        turn_e(5, 1, 1, 0)
+        quantize_e(0, 1)
+        copy_hd(1, 1, 3, 4)
+        turn_e(6, 1, 0, 1)
+        copy_hd(0, 1, 2, 3)
+        quantize_hd(1, 0, 2)
+        copy_e(4, 1, 1, 1)
+        quantize_hd(1, 3, 4)
+        quantize_hd(1, 2, 3)
+        second_product(2, 0, 0, 1, 0, 512)
+        vb_add(2, 1)
+        vb_products("vector", 3, 2)
+        copy_e(3, 1, 0, 0)
+        second_product(1, 0, 2, 3, 0, 512)
+        copy_e(5, 1, 1, 0)
+        second_product(3, 0, 3, 4, 0, 512)
+        subtract(2, 0, 0, 1, 0, 512)
+        vb_add(3, 3)
+        copy_e(6, 1, 0, 1)
+        second_product(0, 0, 1, 2, 0, 512)
+        subtract(1, 0, 2, 3, 0, 512)
+        store_y(0, 0, 1, 0, 512)
+        turn_e(5, 2, 0, 1)
+        subtract(0, 0, 1, 2, 0, 512)
+        vb_add(3, 0)
+        turn_e(6, 2, 0, 0)
+        subtract(3, 0, 3, 4, 0, 512)
+        copy_e(5, 2, 0, 1)
+        store_y(0, 1, 2, 0, 512)
+        store_y(0, 2, 3, 0, 512)
+        turn_e(2, 2, 1, 1)
+        copy_e(6, 2, 0, 0)
+        quantize_e(1, 1)
+        store_y(0, 3, 4, 0, 512)
+        turn_e(4, 2, 1, 0)
+        copy_e(2, 2, 1, 1)
+        quantize_e(1, 0)
+        turn_e(5, 3, 0, 0)
+        copy_e(4, 2, 1, 0)
+        quantize_e(2, 0)
+        second_product(3, 1, 2, 3, 0, 512)
+        copy_e(5, 3, 0, 0)
+        round_y("gpsimd", 0, 256, 512)
+        second_product(0, 1, 0, 1, 0, 512)
+        round_y("scalar", 0, 0, 256)
+        subtract(3, 1, 2, 3, 0, 512)
+        second_product(6, 1, 3, 4, 0, 512)
+        subtract(0, 1, 0, 1, 0, 512)
+        second_product(1, 1, 1, 2, 0, 512)
+        vb_add(3, 2)
+        subtract(6, 1, 3, 4, 0, 512)
+        store_y(1, 0, 1, 0, 512)
+        store_y(1, 2, 3, 0, 512)
+        turn_e(2, 3, 1, 0)
+        store_y(1, 3, 4, 0, 512)
+        turn_e(4, 3, 0, 1)
+        quantize_e(2, 1)
+        copy_e(2, 3, 1, 0)
+        turn_e(0, 3, 1, 1)
+        subtract(1, 1, 1, 2, 0, 512)
+        copy_e(4, 3, 0, 1)
+        second_product(6, 2, 2, 3, 0, 512)
+        quantize_y(0, 0, 256)
+        store_y(1, 1, 2, 0, 512)
+        copy_e(0, 3, 1, 1)
+        quantize_y(0, 256, 512)
+        quantize_e(3, 0)
+        second_product(3, 2, 1, 2, 0, 512)
+        store_words(0, 0, 512)
+        round_y("scalar", 1, 0, 256)
+        second_product(1, 2, 0, 1, 0, 512)
+        quantize_e(3, 1)
+        second_product(5, 2, 3, 4, 0, 512)
+        round_y("gpsimd", 1, 256, 512)
+        subtract(6, 2, 2, 3, 0, 512)
+        second_product(4, 3, 0, 4, 0, 128)
+        subtract(1, 2, 0, 1, 0, 512)
+        store_y(2, 2, 3, 0, 512)
+        subtract(3, 2, 1, 2, 0, 512)
+        second_product(2, 3, 0, 4, 128, 256)
+        store_y(2, 0, 1, 0, 512)
+        subtract(5, 2, 3, 4, 0, 512)
+        second_product(1, 3, 0, 4, 384, 512)
+        store_y(2, 1, 2, 0, 512)
+        subtract(2, 3, 0, 4, 128, 256)
+        store_y(2, 3, 4, 0, 512)
+        round_y("scalar", 2, 0, 256)
+        round_y("gpsimd", 2, 256, 512)
+        second_product(0, 3, 0, 4, 256, 384)
+        subtract(4, 3, 0, 4, 0, 128)
+        store_y(3, 0, 4, 128, 256)
+        subtract(1, 3, 0, 4, 384, 512)
+        store_y(3, 0, 4, 0, 128)
+        quantize_y(1, 0, 256)
+        store_y(3, 0, 4, 384, 512)
+        quantize_y(1, 256, 512)
+        round_y("scalar", 3, 128, 256)
+        quantize_y(2, 256, 512)
+        store_words(1, 0, 512)
+        quantize_y(2, 0, 256)
+        round_y("scalar", 3, 0, 128)
+        subtract(0, 3, 0, 4, 256, 384)
+        store_scales("sync", 3, 0, 3)
+        store_scales("sync", 2, 0, 3)
+        store_scales("sync", 1, 0, 3)
+        store_scales("sync", 0, 0, 3)
+        round_y("scalar", 3, 256, 384)
+        quantize_y(3, 0, 128)
+        quantize_y(3, 128, 256)
+        round_y("vector", 3, 384, 512)
+        store_words(3, 0, 256)
+        store_y(3, 0, 4, 256, 384)
+        quantize_y(3, 384, 512)
+        quantize_y(3, 256, 384)
+        store_words(2, 0, 512)
+        store_scales("sync", 1, 3, 4)
+        store_words(3, 256, 512)
+        store_scales("sync", 3, 3, 4)
+        store_scales("scalar", 2, 3, 4)
+        store_scales("scalar", 0, 3, 4)

@@ -23,8 +23,7 @@ RH = R // 512
 NG = N // 512
 JT = J // P
 VW = J + 1
-SECOND_BUFS = 8
-SORTED = (0, 1,)
+SORTED = (0,)
 H_BANKS = ((2, 3, 4, 5), (6, 0, 1, 2))
 
 
@@ -50,21 +49,21 @@ def tile_golub_kahan_defect_k5_kernel(
         ab_sb = sb("ab_sb", [P, 2 * J], BF16)
         u_w = sb("u_w", [P, KG, 2 * J], U8)
         u_s = sb("u_s", [P, KG, J], U8)
-        f_w = [sb("f_w%d" % h, [P, KG, 1024], U8) for h in range(RH)]
-        f_s = [sb("f_s%d" % h, [P, KG, 512], U8) for h in range(RH)]
+        f_w = sb("f_w", [P, KG, 2 * R], U8)
+        f_s = sb("f_s", [P, KG, R], U8)
         v_sb = [sb("v_sb%d" % g, [P, 4 * VW], BF16) for g in range(NG)]
         e_sb = [sb("e_sb%d" % g, [P, 4, R], BF16) for g in range(NG)]
-        e_codes = [sb("e_codes%d" % g, [P, RH, 512], U32) for g in range(NG)]
-        e_scale = [sb("e_scale%d" % g, [P, RH, 512], U8) for g in range(NG)]
+        e_codes = [sb("e_codes%d" % g, [P, RH * 512], U32) for g in range(NG)]
+        e_scale = [sb("e_scale%d" % g, [P, RH * 512], U8) for g in range(NG)]
         hd_t = [sb("hd_t%d" % jt, [P, R], BF16) for jt in range(JT)]
         hd_in = [sb("hd_in%d" % h, [P, 4 * J], BF16) for h in range(RH)]
         hd_codes = [sb("hd_codes%d" % h, [P, J], U32) for h in range(RH)]
         hd_scale = [sb("hd_scale%d" % h, [P, J], U8) for h in range(RH)]
         y = [sb("y%d" % g, [P, 4, J], F32) for g in range(NG)]
-        second = [sb("second%d" % i, [P, J], F32) for i in range(SECOND_BUFS)]
-        e_in = [sb("e_in%d" % i, [P, 2048], BF16) for i in range(4)]
-        e_sorted = [sb("e_sorted%d" % g, [P, 4, RH, 256], F32) for g in range(2)]
-        y_in = [sb("y_in%d" % i, [P, 256, 4], BF16) for i in range(4)]
+        second = [sb("second%d" % i, [P, 4, J], F32) for i in range(2)]
+        e_in = [sb("e_in%d" % i, [P, 4096], BF16) for i in range(2)]
+        e_sorted = [sb("e_sorted%d" % g, [P, 4, RH, 256], F32) for g in SORTED]
+        y_in = [sb("y_in%d" % g, [P, J, 4], BF16) for g in range(NG)]
         y_codes = sb("y_codes", [P, NG, J], U32)
         y_scale = sb("y_scale", [P, NG, J], U8)
 
@@ -84,26 +83,29 @@ def tile_golub_kahan_defect_k5_kernel(
             src = u_words.bitcast(I32)[g0:g1].rearrange("g p c -> p g c")
             nc.sync.dma_start(out=u_w[:, g0:g1, :].bitcast(I32), in_=src)
 
-        def load_f_words(h, g0, g1):
-            src = f_words.bitcast(I32)[g0:g1, :, 256 * h : 256 * (h + 1)].rearrange("g p c -> p g c")
-            nc.sync.dma_start(out=f_w[h][:, g0:g1, :].bitcast(I32), in_=src)
+        def load_f_words(g0, g1):
+            src = f_words.bitcast(I32)[g0:g1].rearrange("g p c -> p g c")
+            nc.sync.dma_start(out=f_w[:, g0:g1, :].bitcast(I32), in_=src)
 
-        planes = [(u_s, u_scales, 0), (f_s[0], f_scales, 0), (f_s[1], f_scales, 128)]
+        planes = [(u_s, u_scales), (f_s, f_scales)]
 
         def clear_plane(which, g0, g1):
             nc.vector.memset(planes[which][0][:, g0:g1, :].bitcast(I32), 0)
 
         def load_scales(which, g0, g1):
-            plane, scales, c0 = planes[which]
+            plane, scales = planes[which]
             src = scales.bitcast(I32).rearrange("g (q r) c -> r q g c", r=4)
             for r in range(4):
-                nc.sync.dma_start(out=plane[r:P:32, g0:g1, :].bitcast(I32), in_=src[r][:, g0:g1, c0 : c0 + 128])
+                nc.sync.dma_start(out=plane[r:P:32, g0:g1, :].bitcast(I32), in_=src[r][:, g0:g1, :])
 
         def clear_vectors():
             nc.vector.memset(vec_rows[:], 0.0)
 
+        def clear_identity(which):
+            nc.vector.memset((ident_b, ident_f)[which][:], 0.0)
+
         def identity(which):
-            make_identity(nc, (ident_b, ident_f)[which][:])
+            make_identity(nc, (ident_b, ident_f)[which][:], nomemset=True)
 
         turned = banks[0][:].bitcast(BF16)
         ab = banks[7][:].bitcast(BF16)
@@ -115,43 +117,55 @@ def tile_golub_kahan_defect_k5_kernel(
         def copy_vectors():
             nc.scalar.copy(out=vec_cols[:], in_=turned[:, 0:16])
 
-        def spread(which):
+        def spread(which, c0):
             dst = ab if which == 0 else d_ps
-            for c in range(8):
+            for c in range(c0, 8):
                 col = vec_cols[:, 8 * which + c : 8 * which + c + 1]
                 nc.tensor.transpose(dst[:, P * c : P * (c + 1)], col.to_broadcast([P, P]), ident_b[:])
 
         def copy_ab():
             nc.scalar.copy(out=ab_sb[:], in_=ab)
 
-        def copy_d():
-            for h in range(RH):
+        def copy_d(h0):
+            for h in range(h0, RH):
                 nc.scalar.copy(
                     out=d_wide[:, 512 * h : 512 * (h + 1)].rearrange("q (u p e) -> q u p e", u=2, e=2),
                     in_=d_ps[:, 512 * h : 512 * (h + 1)].rearrange("q (p u e) -> q u p e", u=2, e=2),
                 )
 
-        def vb_products(engine, g, t):
-            v0 = v_sb[g][:, VW * t : VW * t + J]
-            v1 = v_sb[g][:, VW * t + 1 : VW * t + 1 + J]
+        def vb_products(engine, g, t0, t1):
+            rows = v_sb[g][:].rearrange("p (t j) -> p t j", t=4)[:, t0:t1, :]
             eng, wide = (nc.gpsimd, ab_sb[:]) if engine == "gpsimd" else (nc.vector, ab)
-            eng.tensor_tensor(out=y[g][:, t, :], in0=v0, in1=wide[:, 0:J], op=MULT)
-            eng.tensor_tensor(out=second[(4 * g + t) % SECOND_BUFS][:], in0=v1, in1=wide[:, J : 2 * J], op=MULT)
+            outs = (y[g][:, t0:t1, :], second[g % 2][:, t0:t1, :])
+            for shift in range(2):
+                factor = wide[:, J * shift : J * (shift + 1)].unsqueeze(1).to_broadcast([P, t1 - t0, J])
+                eng.tensor_tensor(out=outs[shift], in0=rows[:, :, shift : shift + J], in1=factor, op=MULT)
 
-        def vb_add(g, t):
-            nc.gpsimd.tensor_tensor(
-                out=y[g][:, t, :], in0=y[g][:, t, :], in1=second[(4 * g + t) % SECOND_BUFS][:], op=ADD
-            )
+        def vb_add(g, t0, t1):
+            dst = y[g][:, t0:t1, :]
+            nc.gpsimd.tensor_tensor(out=dst, in0=dst, in1=second[g % 2][:, t0:t1, :], op=ADD)
 
-        def first(h, jts, gs):
+        def warm_up(n):
+            for i in range(n):
+                nc.tensor.matmul_mx(
+                    out=banks[6][:],
+                    lhsT=u_w[:, 0, 0:256].bitcast(FP4X4),
+                    lhsT_scale=u_s[:, 0, 0:P],
+                    rhs=u_w[:, 0, :].bitcast(FP4X4),
+                    rhs_scale=u_s[:, 0, :],
+                    start=True,
+                    stop=True,
+                )
+
+        def first(tiles, gs):
             for g in gs:
-                for jt in jts:
+                for h, jt in [divmod(tile, JT) for tile in tiles]:
                     nc.tensor.matmul_mx(
                         out=banks[H_BANKS[h][jt]][:],
                         lhsT=u_w[:, g, 256 * jt : 256 * (jt + 1)].bitcast(FP4X4),
                         lhsT_scale=u_s[:, g, P * jt : P * (jt + 1)],
-                        rhs=f_w[h][:, g, :].bitcast(FP4X4),
-                        rhs_scale=f_s[h][:, g, :],
+                        rhs=f_w[:, g, 1024 * h : 1024 * (h + 1)].bitcast(FP4X4),
+                        rhs_scale=f_s[:, g, 512 * h : 512 * (h + 1)],
                         start=(g == 0),
                         stop=(g == KG - 1),
                     )
@@ -208,25 +222,28 @@ def tile_golub_kahan_defect_k5_kernel(
                     nc.tensor.transpose(banks[b][:, P * slot : P * (slot + 1)], src, ident_f[:])
 
         def copy_e(b, g, h, pair):
-            dst = e_in[(2 * g + h) % 4][:].bitcast(F32)[:, 512 * pair : 512 * (pair + 1)]
+            dst = e_in[g % 2][:].bitcast(F32)[:, 1024 * pair + 512 * h : 1024 * pair + 512 * (h + 1)]
             nc.scalar.copy(
                 out=dst.rearrange("p (i n u) -> p i n u", i=2, u=2),
                 in_=banks[b][:].rearrange("p (i u n) -> p i n u", i=2, u=2),
             )
 
-        def quantize_e(g, h):
+        def quantize_e(g, c0, c1):
             nc.vector.quantize_mx(
-                out=e_codes[g][:, h, :].bitcast(FP8X4), scales=e_scale[g][:, h, :], in_=e_in[(2 * g + h) % 4][:]
+                out=e_codes[g][:, c0:c1].bitcast(FP8X4),
+                scales=e_scale[g][:, c0:c1],
+                in_=e_in[g % 2][:, 4 * c0 : 4 * c1],
             )
 
         def second_product(b, g, t0, t1, j0, j1):
             width = j1 - j0
             for t in range(t0, t1):
                 for h in range(RH):
+                    c0 = 512 * (t // 2) + 256 * h + P * (t % 2)
                     nc.tensor.matmul_mx(
                         out=banks[b][:, width * (t - t0) : width * (t - t0 + 1)],
-                        lhsT=e_codes[g][:, h, P * t : P * (t + 1)].bitcast(FP8X4),
-                        lhsT_scale=e_scale[g][:, h, P * t : P * (t + 1)],
+                        lhsT=e_codes[g][:, c0 : c0 + P].bitcast(FP8X4),
+                        lhsT_scale=e_scale[g][:, c0 : c0 + P],
                         rhs=hd_codes[h][:, j0:j1].bitcast(FP8X4),
                         rhs_scale=hd_scale[h][:, j0:j1],
                         start=(h == 0),
@@ -238,7 +255,7 @@ def tile_golub_kahan_defect_k5_kernel(
             nc.vector.tensor_tensor(out=dst, in0=banks[b][:].rearrange("p (t j) -> p t j", t=t1 - t0), in1=dst, op=SUB)
 
         def round_y(engine, g, j0, j1):
-            dst = y_in[(2 * g + j0 // 256) % 4][:, j0 % 256 : j0 % 256 + j1 - j0, :]
+            dst = y_in[g][:, j0:j1, :]
             src = y[g][:, :, j0:j1].rearrange("p t j -> p j t")
             if engine == "scalar":
                 nc.scalar.copy(out=dst, in_=src)
@@ -248,7 +265,7 @@ def tile_golub_kahan_defect_k5_kernel(
                 nc.gpsimd.tensor_scalar(out=dst, in0=src, scalar1=1.0, scalar2=0.0, op0=MULT, op1=ADD)
 
         def quantize_y(g, j0, j1):
-            src = y_in[(2 * g + j0 // 256) % 4][:, j0 % 256 : j0 % 256 + j1 - j0, :]
+            src = y_in[g][:, j0:j1, :]
             nc.vector.quantize_mx(
                 out=y_codes[:, g, j0:j1].bitcast(FP8X4),
                 scales=y_scale[:, g, j0:j1],
@@ -269,239 +286,201 @@ def tile_golub_kahan_defect_k5_kernel(
             eng.dma_start(out=dst[r][:, g0:g1, :], in_=y_scale[r:P:32, g0:g1, :].bitcast(I32))
 
         clear_vectors()
+        clear_identity(0)
         clear_plane(0, 0, 3)
         load_vector(0)
-        clear_plane(0, 3, 8)
         load_vector(1)
-        load_vector(2)
-        load_u_words(0, 2)
-        clear_plane(1, 3, 8)
-        load_scales(0, 0, 3)
-        clear_plane(1, 0, 3)
-        clear_plane(2, 0, 8)
         identity(0)
-        load_scales(1, 0, 3)
+        load_vector(2)
+        load_v(0)
+        load_scales(0, 0, 3)
+        clear_identity(1)
+        clear_plane(0, 3, 8)
         identity(1)
+        clear_plane(1, 0, 3)
+        clear_plane(1, 3, 8)
+        load_u_words(0, 2)
+        load_scales(1, 0, 3)
         turn_vectors()
         copy_vectors()
-        load_f_words(0, 0, 2)
-        spread(0)
-        load_v(0)
-        load_u_words(2, 4)
-        load_f_words(0, 2, 4)
-        spread(1)
-        copy_ab()
-        load_scales(0, 3, 8)
-        copy_d()
-        load_scales(1, 3, 8)
-        first(0, (0, 1, 2, 3), (0,))
-        vb_products("vector", 0, 1)
-        vb_products("vector", 0, 3)
-        vb_add(0, 1)
-        first(0, (0, 1, 2, 3), (1,))
-        load_u_words(4, 6)
-        load_f_words(0, 4, 6)
+        spread(0, 0)
+        spread(1, 0)
+        vb_products("vector", 0, 2, 4)
+        load_f_words(0, 1)
+        load_f_words(1, 2)
         load_v(1)
-        vb_products("vector", 0, 0)
-        load_u_words(6, 8)
-        vb_add(0, 3)
-        first(0, (0, 1, 2, 3), (2,))
-        load_f_words(0, 6, 8)
-        load_scales(2, 0, 8)
-        vb_products("vector", 0, 2)
-        first(0, (0, 1, 2, 3), (3,))
-        load_f_words(1, 0, 4)
-        vb_add(0, 2)
-        first(0, (0, 1, 2, 3), (4,))
+        copy_d(0)
+        load_u_words(2, 4)
+        warm_up(2)
+        load_f_words(2, 3)
+        load_scales(0, 3, 8)
+        vb_products("vector", 0, 0, 2)
+        vb_add(0, 2, 4)
+        first((0, 4, 1, 5, 2, 6, 3), (0,))
+        load_scales(1, 3, 8)
+        vb_products("vector", 1, 2, 4)
+        vb_add(0, 0, 2)
+        first((0, 4, 1, 5, 2, 6, 3), (1,))
+        load_f_words(3, 4)
         load_v(2)
-        vb_products("vector", 1, 2)
-        vb_add(0, 0)
-        first(0, (0, 1, 2, 3), (5,))
-        load_f_words(1, 4, 8)
-        vb_products("vector", 1, 1)
-        load_e(0)
-        first(0, (3,), (6, 7))
-        vb_add(1, 2)
+        load_u_words(4, 6)
+        vb_products("vector", 1, 0, 2)
+        load_f_words(4, 6)
+        first((0, 4, 1, 5, 2, 6, 3), (2,))
+        vb_add(1, 2, 4)
         load_v(3)
-        first(0, (1,), (6, 7))
+        load_u_words(6, 8)
+        load_f_words(6, 8)
+        load_e(0)
         load_e(1)
-        scale_by_d(0, 3)
+        first((0, 4, 1, 5, 2, 6, 3), (3,))
+        vb_add(1, 0, 2)
         load_e(2)
-        first(0, (2,), (6, 7))
-        vb_add(1, 1)
+        vb_products("vector", 2, 0, 2)
         load_e(3)
-        scale_by_d(0, 1)
-        first(0, (0,), (6, 7))
-        scale_by_d(0, 2)
-        vb_products("gpsimd", 1, 3)
-        scale_by_d(0, 0)
-        first(1, (0, 1, 2, 3), (0,))
-        vb_products("vector", 1, 0)
-        turn_hd(4, 0, 2, 4)
-        turn_hd(3, 0, 0, 2)
-        vb_products("vector", 2, 2)
-        copy_hd(4, 0, 2, 4)
-        first(1, (0, 1, 2, 3), (1,))
-        vb_products("gpsimd", 2, 3)
-        copy_hd(3, 0, 0, 2)
-        vb_products("vector", 2, 1)
-        first(1, (0, 1, 2, 3), (2,))
-        vb_products("vector", 2, 0)
-        first(1, (0, 1, 2, 3), (3,))
-        sort_e(0, 1)
-        vb_add(1, 3)
-        first(1, (3,), (4, 5, 6, 7))
-        vb_products("vector", 3, 3)
+        first((0, 4, 1, 5, 2, 6, 3), (4,))
+        vb_products("vector", 2, 2, 4)
+        vb_add(2, 0, 2)
+        first((0, 4, 1, 5, 2, 6, 3), (5,))
+        vb_products("vector", 3, 0, 2)
+        vb_add(2, 2, 4)
+        first((0,), (6, 7))
+        first((1,), (6, 7))
         sort_e(0, 0)
-        vb_add(2, 2)
-        first(1, (1,), (4, 5, 6, 7))
-        vb_products("vector", 3, 1)
-        vb_add(1, 0)
-        first(1, (0,), (4, 5, 6, 7))
-        sort_e(1, 1)
-        scale_by_d(1, 3)
-        vb_add(2, 3)
+        first((4,), (6, 7))
+        scale_by_d(0, 0)
+        first((5,), (6, 7))
+        vb_add(3, 0, 2)
+        scale_by_d(0, 1)
+        first((2,), (6, 7))
+        sort_e(0, 1)
         scale_by_d(1, 1)
-        first(1, (2,), (4, 5, 6, 7))
-        sort_e(1, 0)
-        quantize_hd(0, 0, 4)
-        turn_e(5, 0, 0, 0)
+        first((3,), (6, 7))
+        scale_by_d(0, 2)
+        first((7,), (0, 1, 2, 3))
+        scale_by_d(0, 3)
         scale_by_d(1, 0)
-        vb_add(3, 1)
-        turn_e(3, 0, 0, 1)
-        copy_e(5, 0, 0, 0)
-        scale_by_d(1, 2)
-        turn_e(4, 0, 1, 0)
-        turn_hd(6, 1, 0, 2)
-        copy_e(3, 0, 0, 1)
-        vb_products("vector", 3, 0)
-        vb_add(2, 0)
+        turn_hd(4, 0, 2, 4)
+        vb_products("vector", 3, 2, 4)
+        turn_e(0, 0, 0, 0)
+        copy_hd(4, 0, 2, 4)
+        turn_hd(6, 0, 0, 2)
+        turn_hd(3, 1, 0, 2)
+        copy_hd(6, 0, 0, 2)
         turn_e(5, 0, 1, 1)
-        turn_hd(1, 1, 3, 4)
-        copy_e(4, 0, 1, 0)
-        turn_hd(0, 1, 2, 3)
-        turn_e(3, 1, 0, 0)
+        first((6,), (6, 7))
+        copy_e(0, 0, 0, 0)
+        first((7,), (4, 5, 6, 7))
         copy_e(5, 0, 1, 1)
-        turn_e(4, 1, 1, 1)
-        quantize_e(0, 0)
-        copy_hd(6, 1, 0, 2)
-        turn_e(5, 1, 1, 0)
-        quantize_e(0, 1)
-        copy_hd(1, 1, 3, 4)
-        turn_e(6, 1, 0, 1)
-        copy_hd(0, 1, 2, 3)
-        quantize_hd(1, 0, 2)
-        copy_e(4, 1, 1, 1)
-        quantize_hd(1, 3, 4)
-        quantize_hd(1, 2, 3)
-        second_product(2, 0, 0, 1, 0, 512)
-        vb_add(2, 1)
-        vb_products("vector", 3, 2)
-        copy_e(3, 1, 0, 0)
-        second_product(1, 0, 2, 3, 0, 512)
-        copy_e(5, 1, 1, 0)
-        second_product(3, 0, 3, 4, 0, 512)
-        subtract(2, 0, 0, 1, 0, 512)
-        vb_add(3, 3)
-        copy_e(6, 1, 0, 1)
-        second_product(0, 0, 1, 2, 0, 512)
-        subtract(1, 0, 2, 3, 0, 512)
-        store_y(0, 0, 1, 0, 512)
-        turn_e(5, 2, 0, 1)
-        subtract(0, 0, 1, 2, 0, 512)
-        vb_add(3, 0)
-        turn_e(6, 2, 0, 0)
-        subtract(3, 0, 3, 4, 0, 512)
-        copy_e(5, 2, 0, 1)
-        store_y(0, 1, 2, 0, 512)
-        store_y(0, 2, 3, 0, 512)
-        turn_e(2, 2, 1, 1)
-        copy_e(6, 2, 0, 0)
-        quantize_e(1, 1)
-        store_y(0, 3, 4, 0, 512)
-        turn_e(4, 2, 1, 0)
-        copy_e(2, 2, 1, 1)
-        quantize_e(1, 0)
-        turn_e(5, 3, 0, 0)
-        copy_e(4, 2, 1, 0)
-        quantize_e(2, 0)
-        second_product(3, 1, 2, 3, 0, 512)
-        copy_e(5, 3, 0, 0)
-        round_y("gpsimd", 0, 256, 512)
-        second_product(0, 1, 0, 1, 0, 512)
-        round_y("scalar", 0, 0, 256)
-        subtract(3, 1, 2, 3, 0, 512)
-        second_product(6, 1, 3, 4, 0, 512)
-        subtract(0, 1, 0, 1, 0, 512)
-        second_product(1, 1, 1, 2, 0, 512)
-        vb_add(3, 2)
-        subtract(6, 1, 3, 4, 0, 512)
-        store_y(1, 0, 1, 0, 512)
-        store_y(1, 2, 3, 0, 512)
-        turn_e(2, 3, 1, 0)
-        store_y(1, 3, 4, 0, 512)
-        turn_e(4, 3, 0, 1)
-        quantize_e(2, 1)
-        copy_e(2, 3, 1, 0)
-        turn_e(0, 3, 1, 1)
-        subtract(1, 1, 1, 2, 0, 512)
-        copy_e(4, 3, 0, 1)
-        second_product(6, 2, 2, 3, 0, 512)
-        quantize_y(0, 0, 256)
-        store_y(1, 1, 2, 0, 512)
-        copy_e(0, 3, 1, 1)
-        quantize_y(0, 256, 512)
-        quantize_e(3, 0)
-        second_product(3, 2, 1, 2, 0, 512)
+        quantize_hd(0, 0, 4)
+        copy_hd(3, 1, 0, 2)
+        scale_by_d(1, 2)
+        vb_add(3, 2, 4)
+        turn_e(6, 0, 1, 0)
+        scale_by_d(1, 3)
+        turn_e(0, 1, 1, 0)
+        copy_e(6, 0, 1, 0)
+        turn_hd(3, 1, 2, 4)
+        copy_e(0, 1, 1, 0)
+        turn_e(1, 0, 0, 1)
+        turn_e(5, 1, 0, 1)
+        copy_hd(3, 1, 2, 4)
+        quantize_e(0, 0, 512)
+        turn_e(2, 1, 0, 0)
+        copy_e(1, 0, 0, 1)
+        turn_e(0, 2, 0, 0)
+        quantize_hd(1, 0, 4)
+        copy_e(2, 1, 0, 0)
+        second_product(4, 0, 1, 2, 0, 512)
+        quantize_e(0, 512, 1024)
+        copy_e(5, 1, 0, 1)
+        second_product(6, 0, 0, 1, 0, 512)
+        quantize_e(1, 0, 512)
+        copy_e(0, 2, 0, 0)
+        second_product(3, 0, 2, 3, 0, 512)
+        subtract(4, 0, 1, 2, 0, 512)
+        second_product(1, 0, 3, 4, 0, 512)
+        subtract(6, 0, 0, 1, 0, 512)
+        turn_e(2, 1, 1, 1)
+        subtract(1, 0, 3, 4, 0, 512)
+        store_y(0, 0, 2, 0, 512)
+        turn_e(6, 2, 1, 0)
+        subtract(3, 0, 2, 3, 0, 512)
+        copy_e(2, 1, 1, 1)
+        turn_e(0, 2, 1, 1)
+        copy_e(6, 2, 1, 0)
+        store_y(0, 2, 4, 0, 512)
+        quantize_e(1, 512, 1024)
+        second_product(4, 1, 0, 1, 0, 512)
+        copy_e(0, 2, 1, 1)
+        round_y("vector", 0, 384, 512)
+        second_product(3, 1, 1, 2, 0, 512)
+        round_y("scalar", 0, 0, 384)
+        subtract(4, 1, 0, 1, 0, 512)
+        second_product(5, 1, 3, 4, 0, 512)
+        subtract(3, 1, 1, 2, 0, 512)
+        second_product(1, 1, 2, 3, 0, 512)
+        quantize_e(2, 0, 512)
+        store_y(1, 0, 2, 0, 512)
+        turn_e(6, 3, 0, 0)
+        subtract(1, 1, 2, 3, 0, 512)
+        turn_e(4, 3, 1, 0)
+        copy_e(6, 3, 0, 0)
+        subtract(5, 1, 3, 4, 0, 512)
+        turn_e(2, 2, 0, 1)
+        copy_e(4, 3, 1, 0)
+        quantize_y(0, 0, 512)
+        second_product(3, 2, 0, 1, 0, 512)
+        store_y(1, 2, 4, 0, 512)
+        copy_e(2, 2, 0, 1)
+        quantize_e(3, 0, 512)
+        second_product(1, 2, 1, 2, 0, 512)
         store_words(0, 0, 512)
-        round_y("scalar", 1, 0, 256)
-        second_product(1, 2, 0, 1, 0, 512)
-        quantize_e(3, 1)
-        second_product(5, 2, 3, 4, 0, 512)
-        round_y("gpsimd", 1, 256, 512)
-        subtract(6, 2, 2, 3, 0, 512)
-        second_product(4, 3, 0, 4, 0, 128)
-        subtract(1, 2, 0, 1, 0, 512)
-        store_y(2, 2, 3, 0, 512)
-        subtract(3, 2, 1, 2, 0, 512)
-        second_product(2, 3, 0, 4, 128, 256)
-        store_y(2, 0, 1, 0, 512)
-        subtract(5, 2, 3, 4, 0, 512)
-        second_product(1, 3, 0, 4, 384, 512)
-        store_y(2, 1, 2, 0, 512)
-        subtract(2, 3, 0, 4, 128, 256)
-        store_y(2, 3, 4, 0, 512)
-        round_y("scalar", 2, 0, 256)
-        round_y("gpsimd", 2, 256, 512)
-        second_product(0, 3, 0, 4, 256, 384)
-        subtract(4, 3, 0, 4, 0, 128)
-        store_y(3, 0, 4, 128, 256)
-        subtract(1, 3, 0, 4, 384, 512)
-        store_y(3, 0, 4, 0, 128)
-        quantize_y(1, 0, 256)
-        store_y(3, 0, 4, 384, 512)
-        quantize_y(1, 256, 512)
-        round_y("scalar", 3, 128, 256)
-        quantize_y(2, 256, 512)
+        round_y("scalar", 1, 0, 384)
+        round_y("vector", 1, 384, 512)
+        turn_e(2, 3, 1, 1)
+        quantize_e(2, 512, 1024)
+        turn_e(5, 3, 0, 1)
+        subtract(1, 2, 1, 2, 0, 512)
+        second_product(6, 2, 3, 4, 0, 512)
+        subtract(3, 2, 0, 1, 0, 512)
+        copy_e(2, 3, 1, 1)
+        second_product(0, 2, 2, 3, 0, 512)
+        subtract(6, 2, 3, 4, 0, 512)
+        store_y(2, 0, 2, 0, 512)
+        copy_e(5, 3, 0, 1)
+        second_product(3, 3, 1, 2, 0, 512)
+        subtract(0, 2, 2, 3, 0, 512)
+        second_product(4, 3, 0, 1, 0, 512)
+        quantize_e(3, 512, 1024)
+        store_y(2, 2, 4, 0, 512)
+        round_y("scalar", 2, 0, 384)
+        subtract(3, 3, 1, 2, 0, 512)
+        second_product(1, 3, 2, 4, 0, 256)
+        subtract(4, 3, 0, 1, 0, 512)
+        second_product(5, 3, 2, 4, 256, 512)
+        subtract(1, 3, 2, 4, 0, 256)
+        store_y(3, 0, 2, 0, 512)
+        round_y("vector", 2, 384, 512)
+        store_y(3, 2, 4, 0, 256)
+        round_y("scalar", 3, 0, 256)
+        quantize_y(1, 0, 512)
+        quantize_y(2, 0, 512)
         store_words(1, 0, 512)
-        quantize_y(2, 0, 256)
-        round_y("scalar", 3, 0, 128)
-        subtract(0, 3, 0, 4, 256, 384)
-        store_scales("sync", 3, 0, 3)
-        store_scales("sync", 2, 0, 3)
-        store_scales("sync", 1, 0, 3)
+        subtract(5, 3, 2, 4, 256, 512)
         store_scales("sync", 0, 0, 3)
+        store_scales("sync", 1, 0, 3)
+        store_scales("sync", 2, 0, 3)
+        store_scales("sync", 3, 0, 3)
+        quantize_y(3, 0, 256)
+        store_y(3, 2, 4, 256, 512)
         round_y("scalar", 3, 256, 384)
-        quantize_y(3, 0, 128)
-        quantize_y(3, 128, 256)
         round_y("vector", 3, 384, 512)
         store_words(3, 0, 256)
-        store_y(3, 0, 4, 256, 384)
-        quantize_y(3, 384, 512)
-        quantize_y(3, 256, 384)
         store_words(2, 0, 512)
-        store_scales("sync", 1, 3, 4)
+        quantize_y(3, 256, 512)
         store_words(3, 256, 512)
+        store_scales("sync", 1, 3, 4)
         store_scales("sync", 3, 3, 4)
-        store_scales("scalar", 2, 3, 4)
         store_scales("scalar", 0, 3, 4)
+        store_scales("scalar", 2, 3, 4)

@@ -23,8 +23,9 @@ RH = R // 512
 NG = N // 512
 JT = J // P
 VW = J + 1
-SORTED = (0,)
+SORTED = (0, 1)
 H_BANKS = ((2, 3, 4, 5), (6, 0, 1, 2))
+V_PITCH = 1040
 
 
 def tile_golub_kahan_defect_k5_kernel(
@@ -46,12 +47,11 @@ def tile_golub_kahan_defect_k5_kernel(
         ident_b = sb("ident_b", [P, P], BF16)
         ident_f = sb("ident_f", [P, P], F32)
         d_wide = sb("d_wide", [P, R], BF16)
-        ab_sb = sb("ab_sb", [P, 2 * J], BF16)
         u_w = sb("u_w", [P, KG, 2 * J], U8)
         u_s = sb("u_s", [P, KG, J], U8)
         f_w = sb("f_w", [P, KG, 2 * R], U8)
         f_s = sb("f_s", [P, KG, R], U8)
-        v_sb = [sb("v_sb%d" % g, [P, 4 * VW], BF16) for g in range(NG)]
+        v_sb = [sb("v_sb%d" % g, [P, 2, V_PITCH], BF16) for g in range(NG)]
         e_sb = [sb("e_sb%d" % g, [P, 4, R], BF16) for g in range(NG)]
         e_codes = [sb("e_codes%d" % g, [P, RH * 512], U32) for g in range(NG)]
         e_scale = [sb("e_scale%d" % g, [P, RH * 512], U8) for g in range(NG)]
@@ -62,8 +62,9 @@ def tile_golub_kahan_defect_k5_kernel(
         y = [sb("y%d" % g, [P, 4, J], F32) for g in range(NG)]
         second = [sb("second%d" % i, [P, 4, J], F32) for i in range(2)]
         e_in = [sb("e_in%d" % i, [P, 4096], BF16) for i in range(2)]
-        e_sorted = [sb("e_sorted%d" % g, [P, 4, RH, 256], F32) for g in SORTED]
-        y_in = [sb("y_in%d" % g, [P, J, 4], BF16) for g in range(NG)]
+        spare = [sb("spare%d" % i, [P, 4096], BF16) for i in range(max(2, len(SORTED)))]
+        e_sorted = [spare[g][:].bitcast(F32).rearrange("n (t h w) -> n t h w", t=4, h=RH) for g in SORTED]
+        y_in = [spare[g // 2][:, 2048 * (g % 2) : 2048 * (g % 2 + 1)].rearrange("p (j t) -> p j t", t=4) for g in range(NG)]
         y_codes = sb("y_codes", [P, NG, J], U32)
         y_scale = sb("y_scale", [P, NG, J], U8)
 
@@ -71,9 +72,9 @@ def tile_golub_kahan_defect_k5_kernel(
             vec, r0, r1 = ((alpha, 0, 4), (beta, 4, 8), (d, 8, 16))[which]
             nc.sync.dma_start(out=vec_rows[r0:r1, :], in_=vec.rearrange("(c p) -> c p", p=P))
 
-        def load_v(g):
-            rows = v[512 * g : 512 * (g + 1), :].rearrange("(p t) j -> p (t j)", t=4)
-            nc.sync.dma_start(out=v_sb[g][:], in_=rows)
+        def load_v(g, pair0, pair1):
+            rows = v[512 * g : 512 * (g + 1), :].rearrange("(p pair t) j -> p pair (t j)", pair=2, t=2)
+            nc.sync.dma_start(out=v_sb[g][:, pair0:pair1, 0 : 2 * VW], in_=rows[:, pair0:pair1, :])
 
         def load_e(g):
             rows = e[512 * g : 512 * (g + 1), :].rearrange("(p t) r -> p t r", t=4)
@@ -123,9 +124,6 @@ def tile_golub_kahan_defect_k5_kernel(
                 col = vec_cols[:, 8 * which + c : 8 * which + c + 1]
                 nc.tensor.transpose(dst[:, P * c : P * (c + 1)], col.to_broadcast([P, P]), ident_b[:])
 
-        def copy_ab():
-            nc.scalar.copy(out=ab_sb[:], in_=ab)
-
         def copy_d(h0):
             for h in range(h0, RH):
                 nc.scalar.copy(
@@ -134,12 +132,11 @@ def tile_golub_kahan_defect_k5_kernel(
                 )
 
         def vb_products(engine, g, t0, t1):
-            rows = v_sb[g][:].rearrange("p (t j) -> p t j", t=4)[:, t0:t1, :]
-            eng, wide = (nc.gpsimd, ab_sb[:]) if engine == "gpsimd" else (nc.vector, ab)
+            rows = v_sb[g][:, t0 // 2, 0 : 2 * VW].rearrange("p (t j) -> p t j", t=2)
             outs = (y[g][:, t0:t1, :], second[g % 2][:, t0:t1, :])
             for shift in range(2):
-                factor = wide[:, J * shift : J * (shift + 1)].unsqueeze(1).to_broadcast([P, t1 - t0, J])
-                eng.tensor_tensor(out=outs[shift], in0=rows[:, :, shift : shift + J], in1=factor, op=MULT)
+                factor = ab[:, J * shift : J * (shift + 1)].unsqueeze(1).to_broadcast([P, t1 - t0, J])
+                nc.vector.tensor_tensor(out=outs[shift], in0=rows[:, :, shift : shift + J], in1=factor, op=MULT)
 
         def vb_add(g, t0, t1):
             dst = y[g][:, t0:t1, :]
@@ -287,200 +284,197 @@ def tile_golub_kahan_defect_k5_kernel(
 
         clear_vectors()
         clear_identity(0)
-        clear_plane(0, 0, 3)
+        clear_identity(1)
         load_vector(0)
         load_vector(1)
-        identity(0)
+        clear_plane(0, 0, 8)
         load_vector(2)
-        load_v(0)
-        load_scales(0, 0, 3)
-        clear_identity(1)
-        clear_plane(0, 3, 8)
-        identity(1)
-        clear_plane(1, 0, 3)
-        clear_plane(1, 3, 8)
+        load_v(0, 0, 2)
         load_u_words(0, 2)
-        load_scales(1, 0, 3)
+        load_f_words(0, 2)
+        identity(0)
+        load_scales(0, 0, 8)
+        clear_plane(1, 0, 4)
+        identity(1)
+        clear_plane(1, 4, 8)
+        load_scales(1, 0, 4)
         turn_vectors()
         copy_vectors()
         spread(0, 0)
         spread(1, 0)
-        vb_products("vector", 0, 2, 4)
-        load_f_words(0, 1)
-        load_f_words(1, 2)
-        load_v(1)
-        copy_d(0)
-        load_u_words(2, 4)
-        warm_up(2)
-        load_f_words(2, 3)
-        load_scales(0, 3, 8)
         vb_products("vector", 0, 0, 2)
+        load_scales(1, 4, 8)
+        copy_d(0)
+        vb_products("vector", 0, 2, 4)
+        warm_up(4)
+        vb_add(0, 0, 2)
+        load_v(1, 0, 2)
+        load_u_words(2, 4)
+        load_f_words(2, 4)
+        load_v(2, 0, 2)
+        load_u_words(4, 8)
         vb_add(0, 2, 4)
         first((0, 4, 1, 5, 2, 6, 3), (0,))
-        load_scales(1, 3, 8)
-        vb_products("vector", 1, 2, 4)
-        vb_add(0, 0, 2)
-        first((0, 4, 1, 5, 2, 6, 3), (1,))
-        load_f_words(3, 4)
-        load_v(2)
-        load_u_words(4, 6)
-        vb_products("vector", 1, 0, 2)
         load_f_words(4, 6)
-        first((0, 4, 1, 5, 2, 6, 3), (2,))
-        vb_add(1, 2, 4)
-        load_v(3)
-        load_u_words(6, 8)
         load_f_words(6, 8)
+        load_v(3, 0, 2)
+        first((0, 4, 1, 5, 2, 6, 3), (1,))
         load_e(0)
+        vb_products("vector", 1, 2, 4)
         load_e(1)
-        first((0, 4, 1, 5, 2, 6, 3), (3,))
-        vb_add(1, 0, 2)
         load_e(2)
-        vb_products("vector", 2, 0, 2)
+        first((0, 4, 1, 5, 2, 6, 3), (2,))
+        vb_products("vector", 1, 0, 2)
+        vb_add(1, 2, 4)
         load_e(3)
-        first((0, 4, 1, 5, 2, 6, 3), (4,))
+        first((0, 4, 1, 5, 2, 6, 3), (3,))
         vb_products("vector", 2, 2, 4)
-        vb_add(2, 0, 2)
+        vb_add(1, 0, 2)
+        first((0, 4, 1, 5, 2, 6, 3), (4,))
+        vb_products("vector", 2, 0, 2)
+        vb_add(2, 2, 4)
         first((0, 4, 1, 5, 2, 6, 3), (5,))
         vb_products("vector", 3, 0, 2)
-        vb_add(2, 2, 4)
-        first((0,), (6, 7))
-        first((1,), (6, 7))
         sort_e(0, 0)
-        first((4,), (6, 7))
-        scale_by_d(0, 0)
-        first((5,), (6, 7))
-        vb_add(3, 0, 2)
-        scale_by_d(0, 1)
         first((2,), (6, 7))
+        vb_add(2, 0, 2)
+        first((5,), (6, 7))
         sort_e(0, 1)
+        first((0,), (6, 7))
+        first((4,), (6, 7))
         scale_by_d(1, 1)
-        first((3,), (6, 7))
-        scale_by_d(0, 2)
-        first((7,), (0, 1, 2, 3))
-        scale_by_d(0, 3)
-        scale_by_d(1, 0)
-        turn_hd(4, 0, 2, 4)
-        vb_products("vector", 3, 2, 4)
+        first((1,), (6, 7))
+        scale_by_d(0, 0)
+        sort_e(1, 0)
+        vb_add(3, 0, 2)
         turn_e(0, 0, 0, 0)
-        copy_hd(4, 0, 2, 4)
-        turn_hd(6, 0, 0, 2)
-        turn_hd(3, 1, 0, 2)
-        copy_hd(6, 0, 0, 2)
-        turn_e(5, 0, 1, 1)
-        first((6,), (6, 7))
+        scale_by_d(1, 0)
+        first((3,), (6, 7))
+        scale_by_d(0, 1)
         copy_e(0, 0, 0, 0)
-        first((7,), (4, 5, 6, 7))
-        copy_e(5, 0, 1, 1)
-        quantize_hd(0, 0, 4)
+        turn_hd(6, 0, 0, 2)
+        vb_products("vector", 3, 2, 4)
+        turn_hd(3, 1, 0, 2)
+        first((6,), (6, 7))
         copy_hd(3, 1, 0, 2)
+        first((7,), (0, 1, 2, 3))
+        copy_hd(6, 0, 0, 2)
+        sort_e(1, 1)
         scale_by_d(1, 2)
         vb_add(3, 2, 4)
-        turn_e(6, 0, 1, 0)
-        scale_by_d(1, 3)
-        turn_e(0, 1, 1, 0)
-        copy_e(6, 0, 1, 0)
-        turn_hd(3, 1, 2, 4)
-        copy_e(0, 1, 1, 0)
+        turn_e(6, 1, 0, 0)
+        scale_by_d(0, 2)
         turn_e(1, 0, 0, 1)
-        turn_e(5, 1, 0, 1)
-        copy_hd(3, 1, 2, 4)
-        quantize_e(0, 0, 512)
-        turn_e(2, 1, 0, 0)
+        scale_by_d(0, 3)
+        turn_e(4, 0, 1, 0)
         copy_e(1, 0, 0, 1)
-        turn_e(0, 2, 0, 0)
-        quantize_hd(1, 0, 4)
-        copy_e(2, 1, 0, 0)
-        second_product(4, 0, 1, 2, 0, 512)
+        turn_e(3, 1, 1, 0)
+        copy_e(4, 0, 1, 0)
+        turn_e(5, 0, 1, 1)
+        turn_e(1, 1, 0, 1)
+        quantize_hd(1, 0, 2)
+        copy_e(5, 0, 1, 1)
+        first((7,), (4, 5, 6, 7))
+        quantize_hd(0, 0, 2)
+        quantize_e(0, 0, 512)
+        copy_e(3, 1, 1, 0)
         quantize_e(0, 512, 1024)
-        copy_e(5, 1, 0, 1)
-        second_product(6, 0, 0, 1, 0, 512)
+        copy_e(1, 1, 0, 1)
+        second_product(0, 0, 0, 2, 0, 256)
+        scale_by_d(1, 3)
+        copy_e(6, 1, 0, 0)
+        second_product(4, 0, 2, 4, 0, 256)
+        turn_e(5, 1, 1, 1)
+        subtract(4, 0, 2, 4, 0, 256)
+        turn_hd(3, 1, 2, 4)
+        copy_e(5, 1, 1, 1)
+        turn_hd(6, 0, 2, 4)
+        subtract(0, 0, 0, 2, 0, 256)
+        turn_e(4, 2, 0, 0)
+        copy_hd(3, 1, 2, 4)
         quantize_e(1, 0, 512)
-        copy_e(0, 2, 0, 0)
-        second_product(3, 0, 2, 3, 0, 512)
-        subtract(4, 0, 1, 2, 0, 512)
-        second_product(1, 0, 3, 4, 0, 512)
-        subtract(6, 0, 0, 1, 0, 512)
-        turn_e(2, 1, 1, 1)
-        subtract(1, 0, 3, 4, 0, 512)
-        store_y(0, 0, 2, 0, 512)
-        turn_e(6, 2, 1, 0)
-        subtract(3, 0, 2, 3, 0, 512)
-        copy_e(2, 1, 1, 1)
-        turn_e(0, 2, 1, 1)
-        copy_e(6, 2, 1, 0)
-        store_y(0, 2, 4, 0, 512)
+        store_y(0, 0, 4, 0, 256)
+        turn_e(1, 2, 1, 0)
+        copy_hd(6, 0, 2, 4)
         quantize_e(1, 512, 1024)
-        second_product(4, 1, 0, 1, 0, 512)
-        copy_e(0, 2, 1, 1)
-        round_y("vector", 0, 384, 512)
-        second_product(3, 1, 1, 2, 0, 512)
-        round_y("scalar", 0, 0, 384)
-        subtract(4, 1, 0, 1, 0, 512)
-        second_product(5, 1, 3, 4, 0, 512)
-        subtract(3, 1, 1, 2, 0, 512)
-        second_product(1, 1, 2, 3, 0, 512)
+        second_product(2, 1, 0, 2, 0, 256)
+        copy_e(4, 2, 0, 0)
+        quantize_hd(1, 2, 4)
+        second_product(0, 1, 2, 4, 0, 256)
+        quantize_hd(0, 2, 4)
+        round_y("scalar", 0, 0, 256)
+        subtract(2, 1, 0, 2, 0, 256)
+        second_product(6, 0, 2, 4, 256, 512)
+        subtract(0, 1, 2, 4, 0, 256)
+        second_product(4, 1, 2, 4, 256, 512)
+        copy_e(1, 2, 1, 0)
+        subtract(6, 0, 2, 4, 256, 512)
+        second_product(5, 0, 0, 2, 256, 512)
+        store_y(1, 0, 4, 0, 256)
+        round_y("scalar", 1, 0, 256)
+        subtract(4, 1, 2, 4, 256, 512)
+        turn_e(2, 2, 1, 1)
+        subtract(5, 0, 0, 2, 256, 512)
+        turn_e(3, 2, 0, 1)
         quantize_e(2, 0, 512)
-        store_y(1, 0, 2, 0, 512)
-        turn_e(6, 3, 0, 0)
-        subtract(1, 1, 2, 3, 0, 512)
-        turn_e(4, 3, 1, 0)
-        copy_e(6, 3, 0, 0)
-        subtract(5, 1, 3, 4, 0, 512)
-        turn_e(2, 2, 0, 1)
-        copy_e(4, 3, 1, 0)
-        quantize_y(0, 0, 512)
-        second_product(3, 2, 0, 1, 0, 512)
-        store_y(1, 2, 4, 0, 512)
-        copy_e(2, 2, 0, 1)
-        quantize_e(3, 0, 512)
-        second_product(1, 2, 1, 2, 0, 512)
-        store_words(0, 0, 512)
-        round_y("scalar", 1, 0, 384)
-        round_y("vector", 1, 384, 512)
-        turn_e(2, 3, 1, 1)
+        copy_e(2, 2, 1, 1)
+        second_product(0, 1, 0, 2, 256, 512)
+        store_y(0, 0, 4, 256, 512)
+        copy_e(3, 2, 0, 1)
+        second_product(6, 2, 0, 1, 0, 512)
+        subtract(0, 1, 0, 2, 256, 512)
+        round_y("scalar", 0, 256, 512)
+        second_product(3, 2, 1, 2, 0, 512)
+        subtract(6, 2, 0, 1, 0, 512)
+        store_y(1, 0, 4, 256, 512)
+        turn_e(0, 3, 1, 1)
+        subtract(3, 2, 1, 2, 0, 512)
+        round_y("scalar", 1, 256, 512)
+        turn_e(1, 3, 0, 0)
         quantize_e(2, 512, 1024)
-        turn_e(5, 3, 0, 1)
-        subtract(1, 2, 1, 2, 0, 512)
-        second_product(6, 2, 3, 4, 0, 512)
-        subtract(3, 2, 0, 1, 0, 512)
-        copy_e(2, 3, 1, 1)
-        second_product(0, 2, 2, 3, 0, 512)
-        subtract(6, 2, 3, 4, 0, 512)
         store_y(2, 0, 2, 0, 512)
-        copy_e(5, 3, 0, 1)
-        second_product(3, 3, 1, 2, 0, 512)
-        subtract(0, 2, 2, 3, 0, 512)
-        second_product(4, 3, 0, 1, 0, 512)
-        quantize_e(3, 512, 1024)
-        store_y(2, 2, 4, 0, 512)
-        round_y("scalar", 2, 0, 384)
-        subtract(3, 3, 1, 2, 0, 512)
-        second_product(1, 3, 2, 4, 0, 256)
-        subtract(4, 3, 0, 1, 0, 512)
-        second_product(5, 3, 2, 4, 256, 512)
-        subtract(1, 3, 2, 4, 0, 256)
-        store_y(3, 0, 2, 0, 512)
-        round_y("vector", 2, 384, 512)
-        store_y(3, 2, 4, 0, 256)
-        round_y("scalar", 3, 0, 256)
+        turn_e(5, 3, 1, 0)
+        quantize_y(0, 0, 512)
+        second_product(4, 2, 2, 3, 0, 512)
+        copy_e(1, 3, 0, 0)
         quantize_y(1, 0, 512)
-        quantize_y(2, 0, 512)
+        store_words(0, 0, 512)
+        turn_e(2, 3, 0, 1)
+        copy_e(5, 3, 1, 0)
+        subtract(4, 2, 2, 3, 0, 512)
+        store_scales("sync", 2, 0, 2)
+        store_scales("sync", 0, 0, 2)
+        second_product(1, 2, 3, 4, 0, 512)
+        copy_e(0, 3, 1, 1)
+        store_scales("sync", 3, 0, 2)
         store_words(1, 0, 512)
-        subtract(5, 3, 2, 4, 256, 512)
-        store_scales("sync", 0, 0, 3)
-        store_scales("sync", 1, 0, 3)
-        store_scales("sync", 2, 0, 3)
-        store_scales("sync", 3, 0, 3)
-        quantize_y(3, 0, 256)
-        store_y(3, 2, 4, 256, 512)
+        store_scales("sync", 1, 0, 2)
+        quantize_e(3, 0, 512)
+        copy_e(2, 3, 0, 1)
+        subtract(1, 2, 3, 4, 0, 512)
+        second_product(6, 3, 1, 2, 0, 512)
+        quantize_e(3, 512, 1024)
+        second_product(5, 3, 0, 1, 0, 512)
+        store_y(2, 2, 4, 0, 512)
+        round_y("scalar", 2, 0, 256)
+        subtract(6, 3, 1, 2, 0, 512)
+        second_product(2, 3, 2, 4, 256, 512)
+        subtract(5, 3, 0, 1, 0, 512)
+        second_product(3, 3, 2, 4, 0, 256)
+        subtract(2, 3, 2, 4, 256, 512)
+        store_y(3, 0, 2, 0, 512)
+        subtract(3, 3, 2, 4, 0, 256)
         round_y("scalar", 3, 256, 384)
+        round_y("vector", 2, 256, 512)
+        store_y(3, 2, 4, 0, 256)
+        store_y(3, 2, 4, 256, 512)
+        round_y("scalar", 3, 0, 256)
         round_y("vector", 3, 384, 512)
-        store_words(3, 0, 256)
+        quantize_y(2, 0, 512)
+        quantize_y(3, 0, 512)
         store_words(2, 0, 512)
-        quantize_y(3, 256, 512)
-        store_words(3, 256, 512)
-        store_scales("sync", 1, 3, 4)
-        store_scales("sync", 3, 3, 4)
-        store_scales("scalar", 0, 3, 4)
-        store_scales("scalar", 2, 3, 4)
+        store_scales("scalar", 2, 2, 4)
+        store_scales("sync", 1, 2, 4)
+        store_scales("sync", 3, 2, 4)
+        store_scales("scalar", 0, 2, 4)
+        store_words(3, 0, 512)

@@ -252,8 +252,8 @@ def tile_golub_kahan_defect_k5_kernel(
             nc.vector.tensor_tensor(out=dst, in0=banks[b][:].rearrange("p (t j) -> p t j", t=t1 - t0), in1=dst, op=SUB)
 
         def round_y(engine, g, j0, j1):
-            dst = y_in[g][:, j0:j1, :]
-            src = y[g][:, :, j0:j1].rearrange("p t j -> p j t")
+            dst = y_in[g][:, j0:j1, :].rearrange("p (c i) t -> p c t i", i=4)
+            src = y[g][:, :, j0:j1].rearrange("p t (c i) -> p c t i", i=4)
             if engine == "scalar":
                 nc.scalar.copy(out=dst, in_=src)
             elif engine == "vector":

from contextlib import ExitStack

import concourse.mybir as mybir
from concourse.masks import make_identity

MA, R, N, J = 4096, 1024, 2048, 512
FLOPS = 2 * MA * R * J + 2 * N * R * J

F32 = mybir.dt.float32
BF16 = mybir.dt.bfloat16
I32 = mybir.dt.int32
U32 = mybir.dt.uint32
U8 = mybir.dt.uint8
FP8X4 = mybir.dt.float8_e4m3fn_x4
FP4X4 = mybir.dt.float4_e2m1fn_x4
MULT = mybir.AluOpType.mult
ADD = mybir.AluOpType.add
SUB = mybir.AluOpType.subtract

P = 128
KG = MA // 512
RH = R // 512
NG = N // 512
JT = J // P
VW = J + 1
SORTED = (0, 1)
H_BANKS = ((2, 3, 4, 5), (6, 0, 1, 2))
V_PITCH = 1040


def tile_golub_kahan_defect_k5_kernel(
    tc, f_words, f_scales, u_words, u_scales, d, e, v, alpha, beta, out_0, out_1, out_2
):
    nc = tc.nc
    with ExitStack() as ctx:
        keep = ctx.enter_context(tc.tile_pool(name="keep", bufs=1))
        psum = ctx.enter_context(tc.psum_pool(name="psum", bufs=1))
        ctx.enter_context(tc.manual_schedule())

        def sb(name, shape, dtype):
            return keep.tile(shape, dtype, name=name, align_bytes=256 if dtype in (U8, U32) else 64)

        banks = [psum.tile([P, 512], F32, name="bank%d" % b) for b in range(8)]

        vec_rows = sb("vec_rows", [P, P], BF16)
        vec_cols = sb("vec_cols", [P, 16], BF16)
        ident_b = sb("ident_b", [P, P], BF16)
        ident_f = sb("ident_f", [P, P], F32)
        d_wide = sb("d_wide", [P, R], BF16)
        u_w = sb("u_w", [P, KG, 2 * J], U8)
        u_s = sb("u_s", [P, KG, J], U8)
        f_w = sb("f_w", [P, KG, 2 * R], U8)
        f_s = sb("f_s", [P, KG, R], U8)
        v_sb = [sb("v_sb%d" % g, [P, 2, V_PITCH], BF16) for g in range(NG)]
        e_sb = [sb("e_sb%d" % g, [P, 4, R], BF16) for g in range(NG)]
        e_codes = [sb("e_codes%d" % g, [P, RH * 512], U32) for g in range(NG)]
        e_scale = [sb("e_scale%d" % g, [P, RH * 512], U8) for g in range(NG)]
        hd_t = [sb("hd_t%d" % jt, [P, R], BF16) for jt in range(JT)]
        hd_in = [sb("hd_in%d" % h, [P, 4 * J], BF16) for h in range(RH)]
        hd_codes = [sb("hd_codes%d" % h, [P, J], U32) for h in range(RH)]
        hd_scale = [sb("hd_scale%d" % h, [P, J], U8) for h in range(RH)]
        y = [sb("y%d" % g, [P, 4, J], F32) for g in range(NG)]
        second = [sb("second%d" % i, [P, 4, J], F32) for i in range(2)]
        e_in = [sb("e_in%d" % i, [P, 4096], BF16) for i in range(2)]
        spare = [sb("spare%d" % i, [P, 4096], BF16) for i in range(max(2, len(SORTED)))]
        e_sorted = [spare[g][:].bitcast(F32).rearrange("n (t h w) -> n t h w", t=4, h=RH) for g in SORTED]
        y_in = [spare[g // 2][:, 2048 * (g % 2) : 2048 * (g % 2 + 1)].rearrange("p (j t) -> p j t", t=4) for g in range(NG)]
        y_codes = sb("y_codes", [P, NG, J], U32)
        y_scale = sb("y_scale", [P, NG, J], U8)

        def load_vector(which):
            vec, r0, r1 = ((alpha, 0, 4), (beta, 4, 8), (d, 8, 16))[which]
            nc.sync.dma_start(out=vec_rows[r0:r1, :], in_=vec.rearrange("(c p) -> c p", p=P))

        def load_v(g, pair0, pair1):
            rows = v[512 * g : 512 * (g + 1), :].rearrange("(p pair t) j -> p pair (t j)", pair=2, t=2)
            nc.sync.dma_start(out=v_sb[g][:, pair0:pair1, 0 : 2 * VW], in_=rows[:, pair0:pair1, :])

        def load_e(g):
            rows = e[512 * g : 512 * (g + 1), :].rearrange("(p t) r -> p t r", t=4)
            nc.sync.dma_start(out=e_sb[g][:], in_=rows)

        def load_u_words(g0, g1):
            src = u_words.bitcast(I32)[g0:g1].rearrange("g p c -> p g c")
            nc.sync.dma_start(out=u_w[:, g0:g1, :].bitcast(I32), in_=src)

        def load_f_words(g0, g1):
            src = f_words.bitcast(I32)[g0:g1].rearrange("g p c -> p g c")
            nc.sync.dma_start(out=f_w[:, g0:g1, :].bitcast(I32), in_=src)

        planes = [(u_s, u_scales), (f_s, f_scales)]

        def clear_plane(which, g0, g1):
            nc.vector.memset(planes[which][0][:, g0:g1, :].bitcast(I32), 0)

        def load_scales(which, g0, g1):
            plane, scales = planes[which]
            src = scales.bitcast(I32).rearrange("g (q r) c -> r q g c", r=4)
            for r in range(4):
                nc.sync.dma_start(out=plane[r:P:32, g0:g1, :].bitcast(I32), in_=src[r][:, g0:g1, :])

        def clear_vectors():
            nc.vector.memset(vec_rows[:], 0.0)

        def clear_identity(which):
            nc.vector.memset((ident_b, ident_f)[which][:], 0.0)

        def identity(which):
            make_identity(nc, (ident_b, ident_f)[which][:], nomemset=True)

        turned = banks[0][:].bitcast(BF16)
        ab = banks[7][:].bitcast(BF16)
        d_ps = banks[1][:].bitcast(BF16)

        def turn_vectors():
            nc.tensor.transpose(turned[:, 0:P], vec_rows[:], ident_b[:])

        def copy_vectors():
            nc.scalar.copy(out=vec_cols[:], in_=turned[:, 0:16])

        def spread(which, c0):
            dst = ab if which == 0 else d_ps
            for c in range(c0, 8):
                col = vec_cols[:, 8 * which + c : 8 * which + c + 1]
                nc.tensor.transpose(dst[:, P * c : P * (c + 1)], col.to_broadcast([P, P]), ident_b[:])

        def copy_d(h0):
            for h in range(h0, RH):
                nc.scalar.copy(
                    out=d_wide[:, 512 * h : 512 * (h + 1)].rearrange("q (u p e) -> q u p e", u=2, e=2),
                    in_=d_ps[:, 512 * h : 512 * (h + 1)].rearrange("q (p u e) -> q u p e", u=2, e=2),
                )

        def vb_products(engine, g, t0, t1):
            rows = v_sb[g][:, t0 // 2, 0 : 2 * VW].rearrange("p (t j) -> p t j", t=2)
            outs = (y[g][:, t0:t1, :], second[g % 2][:, t0:t1, :])
            for shift in range(2):
                factor = ab[:, J * shift : J * (shift + 1)].unsqueeze(1).to_broadcast([P, t1 - t0, J])
                nc.vector.tensor_tensor(out=outs[shift], in0=rows[:, :, shift : shift + J], in1=factor, op=MULT)

        def vb_add(g, t0, t1):
            dst = y[g][:, t0:t1, :]
            nc.gpsimd.tensor_tensor(out=dst, in0=dst, in1=second[g % 2][:, t0:t1, :], op=ADD)

        def warm_up(n):
            for i in range(n):
                nc.tensor.matmul_mx(
                    out=banks[6][:],
                    lhsT=u_w[:, 0, 0:256].bitcast(FP4X4),
                    lhsT_scale=u_s[:, 0, 0:P],
                    rhs=u_w[:, 0, :].bitcast(FP4X4),
                    rhs_scale=u_s[:, 0, :],
                    start=True,
                    stop=True,
                )

        def first(tiles, gs):
            for g in gs:
                for h, jt in [divmod(tile, JT) for tile in tiles]:
                    nc.tensor.matmul_mx(
                        out=banks[H_BANKS[h][jt]][:],
                        lhsT=u_w[:, g, 256 * jt : 256 * (jt + 1)].bitcast(FP4X4),
                        lhsT_scale=u_s[:, g, P * jt : P * (jt + 1)],
                        rhs=f_w[:, g, 1024 * h : 1024 * (h + 1)].bitcast(FP4X4),
                        rhs_scale=f_s[:, g, 512 * h : 512 * (h + 1)],
                        start=(g == 0),
                        stop=(g == KG - 1),
                    )

        def scale_by_d(h, jt):
            cols = slice(512 * h, 512 * (h + 1))
            nc.vector.tensor_tensor(
                out=hd_t[jt][:, cols].rearrange("q (u p e) -> q u p e", u=2, e=2),
                in0=banks[H_BANKS[h][jt]][:].rearrange("q (p u e) -> q u p e", u=2, e=2),
                in1=d_wide[:, cols].rearrange("q (u p e) -> q u p e", u=2, e=2),
                op=MULT,
            )

        def turn_hd(b, h, jt0, jt1):
            for jt in range(jt0, jt1):
                words = hd_t[jt][:, 512 * h : 512 * (h + 1)].bitcast(F32)
                for u in range(2):
                    slot = 2 * (jt - jt0) + u
                    nc.tensor.transpose(
                        banks[b][:, P * slot : P * (slot + 1)], words[:, P * u : P * (u + 1)], ident_f[:]
                    )

        def copy_hd(b, h, jt0, jt1):
            n = jt1 - jt0
            dst = hd_in[h][:].bitcast(F32)[:, 256 * jt0 : 256 * jt1]
            nc.scalar.copy(
                out=dst.rearrange("p (i j u) -> p i j u", i=n, u=2),
                in_=banks[b][:, 0 : 256 * n].rearrange("p (i u j) -> p i j u", i=n, u=2),
            )

        def quantize_hd(h, jt0, jt1):
            nc.vector.quantize_mx(
                out=hd_codes[h][:, P * jt0 : P * jt1].bitcast(FP8X4),
                scales=hd_scale[h][:, P * jt0 : P * jt1],
                in_=hd_in[h][:, 512 * jt0 : 512 * jt1],
            )

        def sort_e(g, h):
            words = e_sb[g][:].bitcast(F32)[:, :, 256 * h : 256 * (h + 1)]
            nc.scalar.copy(
                out=e_sorted[g][:, :, h, :].rearrange("n t (u p) -> n t u p", u=2),
                in_=words.rearrange("n t (p u) -> n t u p", u=2),
            )

        def turn_e(b, g, h, pair):
            for i in range(2):
                t = 2 * pair + i
                for u in range(2):
                    if g in SORTED:
                        src = e_sorted[g][:, t, h, P * u : P * (u + 1)]
                    else:
                        src = e_sb[g][:, t, :].bitcast(F32)[:, 256 * h + u : 256 * (h + 1) : 2]
                    slot = 2 * i + u
                    nc.tensor.transpose(banks[b][:, P * slot : P * (slot + 1)], src, ident_f[:])

        def copy_e(b, g, h, pair):
            dst = e_in[g % 2][:].bitcast(F32)[:, 1024 * pair + 512 * h : 1024 * pair + 512 * (h + 1)]
            nc.scalar.copy(
                out=dst.rearrange("p (i n u) -> p i n u", i=2, u=2),
                in_=banks[b][:].rearrange("p (i u n) -> p i n u", i=2, u=2),
            )

        def quantize_e(g, c0, c1):
            nc.vector.quantize_mx(
                out=e_codes[g][:, c0:c1].bitcast(FP8X4),
                scales=e_scale[g][:, c0:c1],
                in_=e_in[g % 2][:, 4 * c0 : 4 * c1],
            )

        def second_product(b, g, t0, t1, j0, j1):
            width = j1 - j0
            for t in range(t0, t1):
                for h in range(RH):
                    c0 = 512 * (t // 2) + 256 * h + P * (t % 2)
                    nc.tensor.matmul_mx(
                        out=banks[b][:, width * (t - t0) : width * (t - t0 + 1)],
                        lhsT=e_codes[g][:, c0 : c0 + P].bitcast(FP8X4),
                        lhsT_scale=e_scale[g][:, c0 : c0 + P],
                        rhs=hd_codes[h][:, j0:j1].bitcast(FP8X4),
                        rhs_scale=hd_scale[h][:, j0:j1],
                        start=(h == 0),
                        stop=(h == RH - 1),
                    )

        def subtract(b, g, t0, t1, j0, j1):
            dst = y[g][:, t0:t1, j0:j1]
            nc.vector.tensor_tensor(out=dst, in0=banks[b][:].rearrange("p (t j) -> p t j", t=t1 - t0), in1=dst, op=SUB)

        def round_y(engine, g, j0, j1):
            dst = y_in[g][:, j0:j1, :].rearrange("p (c i) t -> p c t i", i=4)
            src = y[g][:, :, j0:j1].rearrange("p t (c i) -> p c t i", i=4)
            if engine == "scalar":
                nc.scalar.copy(out=dst, in_=src)
            elif engine == "vector":
                nc.vector.tensor_copy(out=dst, in_=src)
            else:
                nc.gpsimd.tensor_scalar(out=dst, in0=src, scalar1=1.0, scalar2=0.0, op0=MULT, op1=ADD)

        def quantize_y(g, j0, j1):
            src = y_in[g][:, j0:j1, :]
            nc.vector.quantize_mx(
                out=y_codes[:, g, j0:j1].bitcast(FP8X4),
                scales=y_scale[:, g, j0:j1],
                in_=src.rearrange("p j t -> p (j t)"),
            )

        def store_y(g, t0, t1, j0, j1):
            rows = out_0[512 * g : 512 * (g + 1), :].rearrange("(p t) j -> p t j", t=4)
            nc.sync.dma_start(out=rows[:, t0:t1, j0:j1], in_=y[g][:, t0:t1, j0:j1])

        def store_words(g, j0, j1):
            dst = out_1[g].rearrange("p m t -> p (m t)").bitcast(I32)
            nc.sync.dma_start(out=dst[:, j0:j1], in_=y_codes[:, g, j0:j1].bitcast(I32))

        def store_scales(queue, r, g0, g1):
            dst = out_2.bitcast(I32).rearrange("g (q r) c -> r q g c", r=4)
            eng = nc.scalar if queue == "scalar" else nc.sync
            eng.dma_start(out=dst[r][:, g0:g1, :], in_=y_scale[r:P:32, g0:g1, :].bitcast(I32))

        clear_vectors()
        clear_identity(0)
        clear_identity(1)
        load_vector(0)
        load_vector(1)
        clear_plane(0, 0, 8)
        load_vector(2)
        load_v(0, 0, 2)
        load_u_words(0, 2)
        load_f_words(0, 2)
        identity(0)
        load_scales(0, 0, 8)
        clear_plane(1, 0, 4)
        identity(1)
        clear_plane(1, 4, 8)
        load_scales(1, 0, 4)
        turn_vectors()
        copy_vectors()
        spread(0, 0)
        spread(1, 0)
        vb_products("vector", 0, 0, 2)
        load_scales(1, 4, 8)
        copy_d(0)
        vb_products("vector", 0, 2, 4)
        warm_up(4)
        vb_add(0, 0, 2)
        load_v(1, 0, 2)
        load_u_words(2, 4)
        load_f_words(2, 4)
        load_v(2, 0, 2)
        load_u_words(4, 8)
        vb_add(0, 2, 4)
        first((0, 4, 1, 5, 2, 6, 3), (0,))
        load_f_words(4, 6)
        load_f_words(6, 8)
        load_v(3, 0, 2)
        first((0, 4, 1, 5, 2, 6, 3), (1,))
        load_e(0)
        vb_products("vector", 1, 2, 4)
        load_e(1)
        load_e(2)
        first((0, 4, 1, 5, 2, 6, 3), (2,))
        vb_products("vector", 1, 0, 2)
        vb_add(1, 2, 4)
        load_e(3)
        first((0, 4, 1, 5, 2, 6, 3), (3,))
        vb_products("vector", 2, 2, 4)
        vb_add(1, 0, 2)
        first((0, 4, 1, 5, 2, 6, 3), (4,))
        vb_products("vector", 2, 0, 2)
        vb_add(2, 2, 4)
        first((0, 4, 1, 5, 2, 6, 3), (5,))
        vb_products("vector", 3, 0, 2)
        sort_e(0, 0)
        first((2,), (6, 7))
        vb_add(2, 0, 2)
        first((5,), (6, 7))
        sort_e(0, 1)
        first((0,), (6, 7))
        first((4,), (6, 7))
        scale_by_d(1, 1)
        first((1,), (6, 7))
        scale_by_d(0, 0)
        sort_e(1, 0)
        vb_add(3, 0, 2)
        turn_e(0, 0, 0, 0)
        scale_by_d(1, 0)
        first((3,), (6, 7))
        scale_by_d(0, 1)
        copy_e(0, 0, 0, 0)
        turn_hd(6, 0, 0, 2)
        vb_products("vector", 3, 2, 4)
        turn_hd(3, 1, 0, 2)
        first((6,), (6, 7))
        copy_hd(3, 1, 0, 2)
        first((7,), (0, 1, 2, 3))
        copy_hd(6, 0, 0, 2)
        sort_e(1, 1)
        scale_by_d(1, 2)
        vb_add(3, 2, 4)
        turn_e(6, 1, 0, 0)
        scale_by_d(0, 2)
        turn_e(1, 0, 0, 1)
        scale_by_d(0, 3)
        turn_e(4, 0, 1, 0)
        copy_e(1, 0, 0, 1)
        turn_e(3, 1, 1, 0)
        copy_e(4, 0, 1, 0)
        turn_e(5, 0, 1, 1)
        turn_e(1, 1, 0, 1)
        quantize_hd(1, 0, 2)
        copy_e(5, 0, 1, 1)
        first((7,), (4, 5, 6, 7))
        quantize_hd(0, 0, 2)
        quantize_e(0, 0, 512)
        copy_e(3, 1, 1, 0)
        quantize_e(0, 512, 1024)
        copy_e(1, 1, 0, 1)
        second_product(0, 0, 0, 2, 0, 256)
        scale_by_d(1, 3)
        copy_e(6, 1, 0, 0)
        second_product(4, 0, 2, 4, 0, 256)
        turn_e(5, 1, 1, 1)
        subtract(4, 0, 2, 4, 0, 256)
        turn_hd(3, 1, 2, 4)
        copy_e(5, 1, 1, 1)
        turn_hd(6, 0, 2, 4)
        subtract(0, 0, 0, 2, 0, 256)
        turn_e(4, 2, 0, 0)
        copy_hd(3, 1, 2, 4)
        quantize_e(1, 0, 512)
        store_y(0, 0, 4, 0, 256)
        turn_e(1, 2, 1, 0)
        copy_hd(6, 0, 2, 4)
        quantize_e(1, 512, 1024)
        second_product(2, 1, 0, 2, 0, 256)
        copy_e(4, 2, 0, 0)
        quantize_hd(1, 2, 4)
        second_product(0, 1, 2, 4, 0, 256)
        quantize_hd(0, 2, 4)
        round_y("scalar", 0, 0, 256)
        subtract(2, 1, 0, 2, 0, 256)
        second_product(6, 0, 2, 4, 256, 512)
        subtract(0, 1, 2, 4, 0, 256)
        second_product(4, 1, 2, 4, 256, 512)
        copy_e(1, 2, 1, 0)
        subtract(6, 0, 2, 4, 256, 512)
        second_product(5, 0, 0, 2, 256, 512)
        store_y(1, 0, 4, 0, 256)
        round_y("scalar", 1, 0, 256)
        subtract(4, 1, 2, 4, 256, 512)
        turn_e(2, 2, 1, 1)
        subtract(5, 0, 0, 2, 256, 512)
        turn_e(3, 2, 0, 1)
        quantize_e(2, 0, 512)
        copy_e(2, 2, 1, 1)
        second_product(0, 1, 0, 2, 256, 512)
        store_y(0, 0, 4, 256, 512)
        copy_e(3, 2, 0, 1)
        second_product(6, 2, 0, 1, 0, 512)
        subtract(0, 1, 0, 2, 256, 512)
        round_y("scalar", 0, 256, 512)
        second_product(3, 2, 1, 2, 0, 512)
        subtract(6, 2, 0, 1, 0, 512)
        store_y(1, 0, 4, 256, 512)
        turn_e(0, 3, 1, 1)
        subtract(3, 2, 1, 2, 0, 512)
        round_y("scalar", 1, 256, 512)
        turn_e(1, 3, 0, 0)
        quantize_e(2, 512, 1024)
        store_y(2, 0, 2, 0, 512)
        turn_e(5, 3, 1, 0)
        quantize_y(0, 0, 512)
        second_product(4, 2, 2, 3, 0, 512)
        copy_e(1, 3, 0, 0)
        quantize_y(1, 0, 512)
        store_words(0, 0, 512)
        turn_e(2, 3, 0, 1)
        copy_e(5, 3, 1, 0)
        subtract(4, 2, 2, 3, 0, 512)
        store_scales("sync", 2, 0, 2)
        store_scales("sync", 0, 0, 2)
        second_product(1, 2, 3, 4, 0, 512)
        copy_e(0, 3, 1, 1)
        store_scales("sync", 3, 0, 2)
        store_words(1, 0, 512)
        store_scales("sync", 1, 0, 2)
        quantize_e(3, 0, 512)
        copy_e(2, 3, 0, 1)
        subtract(1, 2, 3, 4, 0, 512)
        second_product(6, 3, 1, 2, 0, 512)
        quantize_e(3, 512, 1024)
        second_product(5, 3, 0, 1, 0, 512)
        store_y(2, 2, 4, 0, 512)
        round_y("scalar", 2, 0, 256)
        subtract(6, 3, 1, 2, 0, 512)
        second_product(2, 3, 2, 4, 256, 512)
        subtract(5, 3, 0, 1, 0, 512)
        second_product(3, 3, 2, 4, 0, 256)
        subtract(2, 3, 2, 4, 256, 512)
        store_y(3, 0, 2, 0, 512)
        subtract(3, 3, 2, 4, 0, 256)
        round_y("scalar", 3, 256, 384)
        round_y("vector", 2, 256, 512)
        store_y(3, 2, 4, 0, 256)
        store_y(3, 2, 4, 256, 512)
        round_y("scalar", 3, 0, 256)
        round_y("vector", 3, 384, 512)
        quantize_y(2, 0, 512)
        quantize_y(3, 0, 512)
        store_words(2, 0, 512)
        store_scales("scalar", 2, 2, 4)
        store_scales("sync", 1, 2, 4)
        store_scales("sync", 3, 2, 4)
        store_scales("scalar", 0, 2, 4)
        store_words(3, 0, 512)
